import numpy as np, ml_dtypes
CORES = [24,25,26,27,28,29,30,31]
N = 8
import mx_ref
BF = ml_dtypes.bfloat16
def gentries(a):
    return np.ascontiguousarray(a.reshape(8, 16, -1).transpose(0, 2, 1)).reshape(8, -1)
def gtable(e):
    e = np.asarray(e); return np.ascontiguousarray(e.reshape(8, -1, 16).transpose(0, 2, 1)).reshape(128, -1).astype(np.int32)
def gcols(t, e):
    v = np.concatenate([t.reshape(8, 16, -1, 4), np.zeros((8, 16, 1, 4), BF)], axis=2)
    return np.ascontiguousarray(np.stack([v[g][:, e[g]] for g in range(8)])).reshape(128, -1)
def tile(rs):
    return np.stack(rs, axis=2).reshape(128, -1).astype(BF)
def cut(t, i, w=512):
    return t[:, w * i:w * i + w]
def pick(q, e):
    c = np.concatenate([q[0].reshape(128, -1, 4), np.zeros((128, 1, 4), np.uint8)], axis=1); s = np.concatenate([q[1], np.ones((16, 1), np.uint8)], axis=1)
    return (np.ascontiguousarray(c[:, e].reshape(128, -1)), np.ascontiguousarray(s[:, e]))
def join(*qs):
    return (np.concatenate([q[0] for q in qs], axis=1), np.concatenate([q[1] for q in qs], axis=1))
def put(q, e, v):
    c, s = q[0].reshape(128, -1, 4).copy(), q[1].copy(); c[:, e] = v[0].reshape(128, -1, 4); s[:, e] = v[1]
    return (c.reshape(128, -1), s)
def pk(c, s):
    return (np.ascontiguousarray(c), mx_ref.live(s))
def emit(q):
    return q[0], q[1]
def packed(v, rng):
    q = [mx_ref.quantize(np.ascontiguousarray(v[r])) for r in range(N)]
    return np.stack([a for a, b in q]), np.stack([mx_ref.plane(b, rng) for a, b in q])
def values_of_codes():
    e, c = np.zeros((128, 128, 4), np.float32), np.zeros((128, 2, 4), np.uint8)
    e[np.arange(128), np.arange(128), 0] = 1
    c[:127, :, 0] = np.arange(256).reshape(2, 128).T[:127]
    return mx_ref.matmul(mx_ref.quantize(e.reshape(128, 512).astype(BF)), (c.reshape(128, 8), np.full((16, 2), 127, np.uint8))).T.reshape(-1).astype(np.float64)
CODE_VALUE, SCALE_VALUE = values_of_codes(), 2.0 ** (np.arange(256) - 127.0)
def decode(q):
    return (CODE_VALUE[q[0]].reshape(16, 8, -1, 4) * SCALE_VALUE[q[1]][:, None, :, None] + 0.0).reshape(128, -1).astype(np.float32)
def f(rng, *shape):
    return mx_ref.flush((rng.standard_normal(shape, dtype=np.float32) * np.exp2(rng.integers(-2, 3, shape[:-1] + (1,)))).astype(BF))
def wide(rng, *shape, cols=0):
    v = rng.standard_normal(shape, dtype=np.float32) * np.exp2(rng.integers(-12, 13, shape)).astype(np.float32)
    if cols: v *= np.repeat(np.exp2(rng.integers(-cols, cols + 1, shape[:-2] + (1, shape[-1] // 4))) * (rng.random(shape[:-2] + (1, shape[-1] // 4)) > 0.0625), 4, axis=-1).astype(np.float32)
    return mx_ref.flush(v.astype(BF))
C, T, S, R = 256, 16, 8, 3
STEP = [1, 2, 4]
def spines(root, right):
    n = np.concatenate([right, np.full((8, 1), C)], axis=1)
    s = [root]
    for i in range(S - 1): s.append(np.take_along_axis(n, s[-1], axis=1))
    return np.stack(s, axis=2).reshape(8, T * S)
def gput(t, e, h):
    a, b = np.concatenate([t.reshape(8, 16, -1, 4), np.zeros((8, 16, 1, 4), BF)], axis=2), h.reshape(8, 16, -1, 4)
    for g in range(8): a[g][:, e[g]] = b[g]
    return np.ascontiguousarray(a[:, :, :C]).reshape(128, -1)
def big(v):
    v = v.astype(np.float32)
    v[np.abs(v) < np.float32(2.0 ** -16)] = 0
    return v.astype(BF)
def numbers_of(rng):
    return {"x": big(f(rng, N, 128, 4 * C)), "u": np.array(f(rng, N, 128, 512)), "v": np.array(f(rng, N, 128, 512))}
def layers(rng):
    return big(f(rng, N, 128, 2048)).reshape(N, 8, 16, 4, 8, 16, 4)
def weights(rng, w):
    c, p = packed(np.ascontiguousarray(w).reshape(N, 128, 2048), rng)
    return {"wc": c, "ws": p}
def signs(rng):
    return rng.permutation(8) % 2 * 2.0 - 1.0
def shape(rng, own, chance, plan=()):
    left, right, n = [C] * C, [C] * C, T
    def hang(h, side, k):
        nonlocal n
        for _ in range(k):
            side[h] = n
            h, side, n = n, right, n + 1
    for m, (a, b, c) in enumerate(plan):
        hang(m, right, a - 1)
        if a > S: hang(n - 1, left, 1)
        hang(m, left, b - 1)
        hang(right[m], left, c - 2)
    way, tree = (rng.random((C, 16)) < chance[own][:, None]).tolist(), own.tolist()
    for j in range(n, C):
        h, i, side = tree[j], 0, (left, right)[way[j][0]]
        while side[h] < C:
            h, i = side[h], i + 1
            side = (left, right)[way[j][i % 16]]
        side[h] = j
    return left, right
def grown(rng):
    return shape(rng, rng.integers(0, T, C), rng.choice([0.3, 0.6, 0.8, 0.95], T))
def places(rng):
    return np.argsort(rng.random((N, 8, C)), axis=2)
def links(e, a):
    t = np.zeros((2, N, 8, C), np.int64)
    for r in range(N):
        for g in range(8):
            p = np.append(e[r, g], C)
            for i in range(2): t[i, r, g, e[r, g]] = p[a[r][g][i]]
    return {"ro": np.stack([gtable(e[r, :, :T]) for r in range(N)]), "le": np.stack([gtable(q) for q in t[0]]), "ri": np.stack([gtable(q) for q in t[1]])}
def forests(rng):
    return links(places(rng), [[grown(rng) for g in range(8)] for r in range(N)])
def setup_inputs(rng):
    return {**numbers_of(rng), **weights(rng, layers(rng)), **forests(rng)}
def setup_inputs_ties(rng):
    d = numbers_of(rng)
    e = rng.permutation(N)
    x = d["x"].reshape(N, 8, 16, C, 4)
    a = x[0][:, :8, :3].copy()
    a[:, :, 2] = 0
    for r in range(N):
        k = np.zeros(C, int) if r == e[0] else rng.permutation(C) % 3
        x[r][:, :8] = a[:, :, k]
    x[e[1]][:, :8] = 0
    u = d["u"].reshape(N, 8, 16, 8, 16, 4)
    k = u[0].copy()
    u[:, :, :, :, 0] = 0
    for g in range(8): u[:, g, :8, g, 0] = k[g, :8, g, 0]
    w = layers(rng)
    w[:, :, :, :, :, :8] = 0
    return {"x": x.reshape(N, 128, 4 * C), "u": u.reshape(N, 128, 512), "v": d["v"], **weights(rng, w), **forests(rng)}
def setup_inputs_near(rng):
    d = numbers_of(rng)
    k = forests(rng)
    x = np.zeros((N, 8, 16, C, 4), np.float32)
    u = d["u"].reshape(N, 128, 128, 4)
    u[:, :, ::16] = 0
    c, half = signs(rng), int(rng.integers(2))
    for r in range(N):
        low, up = 2 * r // N == half, int((r & STEP[0]) > 0)
        root = gentries(k["ro"][r])
        i = rng.integers(0, S, (8, C + 1))
        np.put_along_axis(i, spines(root, gentries(k["ri"][r])), np.arange(T * S)[None] % S, axis=1)
        s = (i[:, :C] + 1 + (0 if low else S * up)) // 2
        size = 2.0 ** -6 if low else 1.0
        x[r, :, 0, :, 0] = ((8 * c + up) * 2.0 ** -30 if low else c)[:, None]
        x[r, :, 8] = ((s[:, :, None] >> np.arange(4)) & 1) * np.exp2(np.arange(4) - 23.0) * size
        x[r, :, 10:] = rng.integers(4, 8, (8, 6, C, 4)) * 2.0 ** -20 * size
        if not low:
            for g in rng.permutation(8)[:4]: x[r, g, 0, root[g, rng.integers(T)], 0] *= np.float32(2.0 ** 30)
        for h in range(0, 128, 16):
            u[r, h, h, 0] = 2.0 ** -30 if low else 1.0
            u[r, h + 8, h] = 2.0 ** -30 if low else 1.0
    w = layers(rng)
    w[:, :, :10] = 0
    w[:, :, :, :, :, :10] = 0
    return {"x": x.reshape(N, 128, 4 * C).astype(BF), "u": u.reshape(N, 128, 512), "v": d["v"], **weights(rng, w), **k}
def setup_inputs_huge(rng):
    d = numbers_of(rng)
    e, a = places(rng), [grown(rng) for r in range(N)]
    x = 0.6 + 0.2 * rng.random((N, 8, 16, C, 4))
    half = int(rng.integers(2))
    for r in range(N):
        c = rng.permutation(C) % 2 if 2 * r // N != half else np.zeros(C, int)
        for g in range(8): x[r, g][:, e[r, g]] *= np.where(c > 0, 2.0 ** 29, -2.0 ** 30)[None, :, None]
    u = d["u"].reshape(N, 128, 128, 4)
    k = 2.0 ** 30 * (1 - 0.25 * rng.random((N, 128, 8, 4))) * signs(rng)[None, None, :, None]
    u[:, :, ::16] = k.astype(np.float32).astype(BF)
    w = np.zeros((N, 128, 4, 128, 4), np.float32)
    i = np.arange(128)
    for b in range(4): w[:, i, b, i, b] = 4
    return {"x": x.astype(np.float32).reshape(N, 128, 4 * C).astype(BF), "u": u.reshape(N, 128, 512), "v": d["v"], **weights(rng, w.astype(BF)), **links(e, [[a[r]] * 8 for r in range(N)])}
def setup_inputs_slots(rng):
    n = [(S + 1,) * 3] * 2 + [(S,) * 3] * 2 + [(S - 1,) * 3] + [(1, 1, 1)] * 3 + [(1, S, 1), (S, 1, 2)]
    h = rng.permutation(8)
    a = []
    for r in range(N):
        odd = bin(r).count("1") % 2
        a.append([])
        for g in range(8):
            o = rng.permutation(10)
            if g == h[0]: o = np.arange(10)
            if g == h[1]: o = (np.arange(10) + 5 * odd) % 10
            a[r].append(shape(rng, rng.integers(10, T, C), rng.choice([0.3, 0.6, 0.8, 0.95], T), [n[i] for i in o]))
    return {**numbers_of(rng), **weights(rng, layers(rng)), **links(places(rng), a)}
def setup_inputs_spread(rng):
    d = setup_inputs(rng)
    d["x"] = big(wide(rng, N, 128, 4 * C, cols=6))
    return d
def check_inputs(d):
    b = []
    for k in ("x", "u", "v"):
        a = np.abs(d[k].astype(np.float32))
        if not (np.isfinite(a).all() and ((a == 0) | (a >= 2.0 ** -30) & (a <= 2.0 ** 30)).all()): b.append("a value of " + k)
    none, least, most = [emit(mx_ref.quantize(np.full((128, 16), k, np.float32).astype(BF)))[1][0, 0] for k in (0.0, 2.0 ** -30, 2.0 ** 30)]
    for r in range(N):
        if ((d["wc"][r] == 0x7F) | (d["wc"][r] == 0xFF)).any(): b.append("wc: a code that is no number")
        s = mx_ref.live(d["ws"][r])
        if ((s != none) & ((s < least) | (s > most))).any(): b.append("ws: a scale out of range")
        root, left, right = [gentries(d[k][r]) for k in ("ro", "le", "ri")]
        if (root < 0).any() or (root >= C).any() or (left < 0).any() or (left > C).any() or (right < 0).any() or (right > C).any():
            b.append("an entry of ro, le or ri out of range")
            continue
        for g in range(8):
            k = np.bincount(np.concatenate([root[g], left[g], right[g]]), minlength=C + 1)
            if (k[:C] != 1).any(): b.append("a place that isn't once a root or a child")
            up = np.arange(C + 1)
            up[left[g]] = np.arange(C)
            up[right[g]] = np.arange(C)
            up[root[g]] = root[g]
            up[C] = C
            for i in range(10): up = up[up]
            if not np.isin(up[:C], root[g]).all(): b.append("a place that no root reaches")
    return b
def reference(x, u, v, wc, ws, ro, le, ri):
    qu = [mx_ref.quantize(u[r]) for r in range(N)]
    lay = [pk(wc[r], ws[r]) for r in range(N)]
    now = [x[r] for r in range(N)]
    root, left, right = [[gentries(a[r]) for r in range(N)] for a in (ro, le, ri)]
    for t in range(R):
        s, sent, score = [], [], []
        for r in range(N):
            s.append(spines(root[r], right[r]))
            sent.append(mx_ref.quantize(gcols(now[r], s[r])))
            score.append(mx_ref.matmul(qu[r], sent[r])[::16].reshape(8, T, S))
        came = decode(join(*sent)).astype(BF)
        for r in range(N):
            lo, hi = min(r, r ^ STEP[t]), max(r, r ^ STEP[t])
            full = [(s[i] < C).reshape(8, T, S) for i in (lo, hi)]
            key = np.concatenate([score[lo], score[hi]], axis=2) + np.float32(0.0)
            o = np.lexsort((-key, ~np.concatenate(full, axis=2)), axis=2)
            first = np.sum(full[0], axis=2, keepdims=True) * int(r == hi)
            a = np.take_along_axis(o, first + np.arange(S), axis=2)
            a = a // S * (T * S) + S * np.arange(T)[:, None] + a % S
            a = np.where(full[int(r == hi)], a, -1)
            n = np.concatenate([a[:, :, 1:], np.full((8, T, 1), -1)], axis=2)
            n = np.where(n < 0, a, n)
            both = np.concatenate([cut(came, lo, 4 * T * S), cut(came, hi, 4 * T * S)], axis=1)
            e = gcols(both, a.reshape(8, -1)).astype(np.float32)
            z = ((e + gcols(both, n.reshape(8, -1)).astype(np.float32)) * np.float32(0.5)).astype(BF)
            q = mx_ref.quantize(z)
            h = tile([np.maximum(mx_ref.matmul(pick(lay[r], np.arange(128 * b, 128 * b + 128)), q), np.float32(0.0)) * np.float32(0.03125) + e[:, b::4] for b in range(4)])
            now[r] = gput(now[r], s[r], h)
            m = np.zeros((8, C + 1), bool)
            np.put_along_axis(m, s[r], True, axis=1)
            m = m[:, :C]
            left[r], right[r] = np.where(m, right[r], left[r]), np.where(m, left[r], right[r])
    y, ol = np.zeros((N, 128, C), np.float32), np.zeros((N, 8, 2 * C), np.float32)
    oc, osc = np.zeros((N, 128, 4 * C), np.uint8), np.zeros((N, 16, C), np.uint8)
    for r in range(N):
        q = mx_ref.quantize(now[r])
        y[r] = mx_ref.matmul(mx_ref.quantize(v[r]), q)
        ol[r] = np.concatenate([left[r], right[r]], axis=1)
        oc[r], osc[r] = emit(q)
    return {"y": y, "ol": ol, "oc": oc, "osc": osc}

@@ -1,0 +1,714 @@
+from concourse.bass import DstId, RemoteDMATransfer
+from concourse.mybir import dt, AluOpType, AxisListType, ActivationFunctionType
+
+BF, F32, I32, U16, X4, U8 = "bfloat16", "float32", "int32", "uint16", "float8_e4m3fn_x4", "uint8"
+PL = 624
+TB = 257
+STEP = [1, 2, 4]
+FAST = [2, 1]
+LAST = ["SSSV", "SSVV"]
+PACE = {"c": 0.00104, "g": 0.00162, "s": 0.00395, "p": 0.0006, "wake": 0.07, "l": 2.0, "r": 2.3, "i": 0.5, "first": 2.0, "d": 0.1, "D": 1.0}
+AHEAD = 0.4
+TRIES = 2000
+PACES = [{}, {"c": 0.00083, "g": 0.001, "s": 0.0016, "p": 0.00045, "wake": 0.04, "l": 1.7, "r": 1.5, "i": 0.3, "first": 1.0},
+         {"c": 0.00124, "g": 0.0024, "s": 0.0065, "p": 0.0009, "wake": 0.1}, {"r": 3.2, "i": 1.0, "first": 3.0, "l": 2.4, "D": 1.5},
+         {"wake": 0.15, "d": 0.3, "l": 2.3}]
+
+_S = {
+    I32: "lw 36 pi 4 pj 4 gt1 20 gt2 20",
+    U16: "goff 18 bl 32 gl 16 upl 8 minl 16 maxl 16 inv0 16 inv1 16 rof 8 sp 26 wo 8 ob2 8 off 72 so 24 fo 16",
+    F32: "pf 8 ci 16 plc 16 c14 16 c2 2 zb 16 r4 4 cpa 26 dum 26 ot 4 kk 48 kr 12 km 384 ks 384 kq 16 pen 26 e99 26 fn 26 pa 26 pn 26 "
+         "fb 24 fi 4 kx 256 rk 16 bef 16 rf 128 rb 512 val 336 iw 512 s1 26 s2 26 s3 26 tw 32 wr 32 ff 80 ow 32 olt 32 ys 256",
+    BF: "kper 128 mask 128 sin 544 p32 512 p16 128 pp 256 pr 256 dif 256 ones 516 hot 516 sb 512 sbl 512 str 544 stl 512 tt 772 mk 352 sc 352 "
+        "xi 1024 ut 512 vt 512 bt0 512 bt1 512 bt2 512 zt0 512 zt1 512 xt 1024 pin 256 pe 768 gm 256 gs 256 rw 96 nm 768 iv 768 "
+        "dh0 1024 dh1 1024 dh2 1024 ef 128 ei 128 hr 64 eh0 384 eh1 448 eh2 512",
+    X4: "qe 512 qw 512 qb 384 qu 128 qu2 128 qv 128 qr 384 qz 256 qx 256 lq0 144 lq1 144 lq2 144",
+    U8: "sw 512 spl 896 su 128 su2 128 sv 128 sr 384 sz 256 sx 256 ls0 576 ls1 576 ls2 576",
+}
+SCRATCH = {k: ("sbuf", [128, int(w)], d) for d, s in _S.items() for k, w in zip(s.split()[::2], s.split()[1::2])}
+SCRATCH["xp"] = ("sbuf", [128, 4, PL], F32)
+SCRATCH["ps"] = ("psum", [128, 4096], F32)
+SEMAPHORES = ["cV", "cS", "cP", "cG"] + ["d%d" % i for i in range(28)] + ["l%d" % i for i in range(12)] + \
+    ["a%s%d" % (k, t) for k in "bkrs" for t in range(3)]
+
+
+def timed(ops, sent, pace):
+    busy = [o["busy"][0] + o["busy"][2] * pace[o["busy"][1]] for o in ops]
+    lag = [pace[o["lag"][0]] + o["lag"][1] if o["lag"] else 0.0 for o in ops]
+    edges = [[] for _ in ops]
+    for k, o in enumerate(ops):
+        for d in o["deps"]:
+            if isinstance(d, tuple):
+                edges[k].append((sent[d[1]], lag[sent[d[1]]]) if d[0] == "a" else (d[1], 0.0))
+            else:
+                edges[k].append((d, lag[d] + pace["wake"]))
+        edges[k].sort()
+    return busy, lag, edges
+
+
+def arrange(ops, sent):
+    n = len(ops)
+    busy, lag, edges = timed(ops, sent, PACE)
+    later = [[] for _ in ops]
+    for k in range(n):
+        for d, w in edges[k]:
+            later[d].append((k, w))
+    chain, left = [None] * n, [len(e) for e in later]
+    todo = [k for k in range(n) if not left[k]]
+    while todo:
+        k = todo.pop()
+        chain[k] = ops[k]["up"] + busy[k] + max([lag[k]] + [w + chain[j] for j, w in later[k]])
+        for d, w in edges[k]:
+            left[d] -= 1
+            if not left[d]:
+                todo.append(d)
+    free, done, plan = {q: 0.0 for q in "VSPGY"}, {}, []
+    ready = {q: {} for q in free}
+    left = [len(e) for e in edges]
+    for k in range(n):
+        if not left[k]:
+            ready[ops[k]["eng"]][k] = 0.0
+    while len(plan) < n:
+        now, eng = min((max(free[q], min(r.values())), q) for q, r in ready.items() if r)
+        mine = ready[eng]
+        k = min((k for k in mine if mine[k] <= now), key=lambda k: (-chain[k], k))
+        soon = [j for j in mine if chain[j] > chain[k] + busy[k] and mine[j] < now + AHEAD * busy[k]]
+        if soon:
+            k = min(soon, key=lambda j: (mine[j], j))
+        done[k] = free[eng] = max(now, mine.pop(k)) + busy[k]
+        plan.append(k)
+        for j, w in later[k]:
+            left[j] -= 1
+            if not left[j]:
+                ready[ops[j]["eng"]][j] = max(done[d] + x for d, x in edges[j])
+    return plan
+
+
+def clock(eng, times, plan):
+    busy, lag, edges = times
+    free, last, done, why, end, k0 = dict.fromkeys("VSPGY", 0.0), {}, {}, {}, 0.0, None
+    for k in plan:
+        e = eng[k]
+        s, w, q = free[e], last.get(e), True
+        for d, x in edges[k]:
+            if done[d] + x > s:
+                s, w, q = done[d] + x, d, False
+        done[k] = free[e] = s + busy[k]
+        last[e], why[k] = k, (w, q)
+        if done[k] + lag[k] > end:
+            end, k0 = done[k] + lag[k], k
+    pairs = []
+    while k0 is not None:
+        w, q = why[k0]
+        if q and w is not None:
+            pairs.append((w, k0))
+        k0 = w
+    return end, pairs
+
+
+def polish(ops, sent, plan):
+    eng = [o["eng"] for o in ops]
+    times = [timed(ops, sent, {**PACE, **p}) for p in PACES]
+    pre = [set(d for d, x in e) for e in times[0][2]]
+    now = [clock(eng, t, plan) for t in times]
+    base = [x[0] for x in now]
+    best, s = float(len(now)), 1
+    for it in range(TRIES):
+        r = []
+        for _ in range(3):
+            s = (s * 1103515245 + 12345) % 2147483648
+            r.append(s >> 8)
+        pairs = now[r[0] % len(now)][1]
+        j, k = pairs[r[1] % len(pairs)]
+        a, b = plan.index(j), plan.index(k)
+        moved, keep, late = {j}, [], [j]
+        for x in plan[a + 1:b]:
+            if pre[x] & moved:
+                moved.add(x)
+                late.append(x)
+            else:
+                keep.append(x)
+        if pre[k] & moved:
+            continue
+        tail, more, t = plan[b + 1:], r[2] % 6, 0
+        while more and t < len(tail) and not pre[tail[t]] & moved:
+            more -= eng[tail[t]] == eng[k]
+            t += 1
+        new = plan[:a] + keep + [k] + tail[:t] + late + tail[t:]
+        then = [clock(eng, x, new) for x in times]
+        c = sum(x[0] / y for x, y in zip(then, base))
+        if c <= best + 0.0015 * max(0.0, 1 - 1.3 * it / TRIES):
+            plan, now, best = new, then, c
+    return plan
+
+
+def rank_program(g, core, T, topo):
+    rank = T.rank_of(core)
+    if rank is None:
+        return
+    op_, act_ = AluOpType, ActivationFunctionType
+    queue = {"V": g.vector, "S": g.scalar, "P": g.tensor, "G": g, "Y": g.sync}
+    ops, past, nxt, arrive, sent = [], {}, {"d": 0, "l": 0, "send": None}, {}, {}
+
+    def A(name, lo=0, hi=None, st=1):
+        hi = SCRATCH[name][1][1] if hi is None else hi
+        cols = frozenset([lo // 512]) if name == "ps" else frozenset(range(lo, hi, st))
+        return (T[name][:, lo:hi:st], [(name, cols)], len(range(lo, hi, st)), False)
+
+    def plane(b, lo, hi):
+        return (T.xp[:, b, lo:hi], [("xp", frozenset(range(PL * b + lo, PL * b + hi)))], hi - lo, False)
+
+    def planes(lo, hi):
+        return (T.xp[:, :, lo:hi], [r for b in range(4) for r in plane(b, lo, hi)[1]], 4 * (hi - lo), False)
+
+    def ind(win, off, words=False):
+        w = win[0].bitcast(dt.uint32) if words else win[0]
+        return (w.indirect(off[0]), win[1] + off[1], 16 * off[2], True)
+
+    def issue(eng, call, outs, ins, busy, lag=None, sem=None, n=1, after=(), quiet=(), up=0.0):
+        deps = set(after)
+        for regs, write in ((outs, True), (ins, False), (quiet, False)):
+            for name, cols in regs:
+                for c, w, who, e in past.get(name, []):
+                    if (write or w or (name == "ps" and e != eng)) and not cols.isdisjoint(c):
+                        deps.add(who)
+        k = len(ops)
+        ops.append({"eng": eng, "call": call, "deps": deps, "busy": busy, "lag": lag, "sem": sem, "n": n, "up": up})
+        for regs, write in ((outs, True), (ins, False)):
+            for name, cols in regs:
+                past.setdefault(name, []).append((cols, write, k, eng))
+        return k
+
+    def urgent(x):
+        ops[-1]["up"] = x
+
+    def half(*os):
+        return 0.5 if all(SCRATCH[o[1][0][0]][2] in (BF, U16) for o in os) else 1
+
+    def span(i, f):
+        return (0.06, "g", i[2]) if i[3] else (0.0, "c", max(64.0, i[2] * f))
+
+    def run(eng, f, outs, ins, busy, after=()):
+        regs = [r for o in ins if isinstance(o, tuple) for r in o[1]]
+        issue(eng, lambda s: f().then_inc(T.sem[s], 1), [r for o in outs for r in o[1]], regs, busy, after=after)
+
+    def ap(o):
+        return o[0] if isinstance(o, tuple) else o
+
+    def cp(o, i):
+        run("V", lambda: g.vector.tensor_copy(o[0], i[0]), [o], [i], span(i, half(o, i)))
+
+    def ms(o, c):
+        run("V", lambda: g.vector.memset(o[0], c), [o], [], span(o, half(o)))
+
+    def ts(o, i, s1, op0, s2=None, op1=None):
+        w = span(i, half(o, i))
+        if op1 is None:
+            run("V", lambda: g.vector.tensor_scalar(o[0], i[0], ap(s1), None, op0), [o], [i, s1], w)
+        else:
+            run("V", lambda: g.vector.tensor_scalar(o[0], i[0], ap(s1), ap(s2), op0, op1), [o], [i, s1, s2], w)
+
+    def tt(o, a, b, op):
+        run("V", lambda: g.vector.tensor_tensor(o[0], a[0], b[0], op), [o], [a, b], span(a, 1 if a[1][0][0] == "ps" else 2))
+
+    def scan(o, keep, add):
+        run("V", lambda: g.vector.tensor_tensor_scan(o[0], keep[0], add[0], 0.0, op_.mult, op_.add), [o], [keep, add],
+            span(add, half(o, keep, add)))
+
+    def red(o, i):
+        run("V", lambda: g.vector.tensor_reduce(o[0], i[0], AxisListType.X, op_.add), [o], [i], span(i, 1))
+
+    def turn(o, i):
+        run("V", lambda: g.vector.transpose(o[0], i[0]), [o], [i], span(i, half(o, i)))
+
+    def quant(q, s, i):
+        run("V", lambda: g.vector.quantize_mx(q[0], s[0], i[0]), [q, s], [i], (0.015, "c", 0.27 * i[2]))
+
+    def act(o, i, func=act_.Copy, scale=None, bias=None):
+        kw = {}
+        if scale is not None:
+            kw["scale"] = scale
+        if bias is not None:
+            kw["bias"] = ap(bias)
+        run("S", lambda: g.scalar.activation(o[0], i[0], func, **kw), [o], [i, bias], span(i, 1))
+
+    def fill(o, c):
+        act(o, A("ones", 0, o[2]), scale=c)
+
+    def mul(eng, o, i, c):
+        if eng == "S":
+            act(o, i, act_.Copy, scale=c)
+        else:
+            ts(o, i, c, op_.mult)
+
+    def mm(bank, lq, ls, rq, rs):
+        o = A("ps", 512 * bank, 512 * bank + 128)
+        run("P", lambda: g.tensor.matmul_mx(o[0], lq[0], ls[0], rq[0], rs[0], True, True), [o], [lq, ls, rq, rs], (0.0, "p", 144))
+
+    def iota(o, pat, base=0, ch=0, whole=False, after=()):
+        kw = {} if whole else {"allow_small_or_imprecise_dtypes": True}
+        run("G", lambda: g.iota(o[0], pat, base, ch, **kw), [o], [], (0.13, "c", 2 * o[2]), after)
+
+    def dma(eng, out, in_, outs=(), ins=(), more=0.0, quiet=(), **kw):
+        s = "d%d" % nxt["d"]
+        nxt["d"] += 1
+        issue(eng, lambda sem: queue[eng].dma_start(out, in_, **kw).then_inc(T.sem[sem], 16), list(outs), list(ins),
+              (0.0, "D" if eng == "G" else "d", 1), ("l", more), s, 16, [("q", nxt["send"])] if eng == "G" else [], quiet)
+
+    def load(eng, o, src, more=0.0, quiet=()):
+        dma(eng, o[0], src, outs=o[1], more=more, quiet=quiet)
+
+    def raw(o):
+        return (o[0].bitcast(dt.uint8), o[1])
+
+    mate = [T.cores[rank ^ s] for s in STEP]
+    low = [rank < (rank ^ s) for s in STEP]
+    own = [0 if lo else 8 for lo in low]
+
+    def send(t, kind, pairs, more):
+        rid, pid = topo.addr(mate[t])[:2]
+        eng = topo.engines(core, mate[t])
+        k = len(eng) // len(pairs)
+        far = T.sem["a%s%d" % (kind, t)]
+        s = "l%d" % nxt["l"]
+        nxt["l"] += 1
+        if len(pairs) == 1:
+            call = lambda sem: g.remote_dma(pairs[0][0][0], pairs[0][1][0], far, T.sem[sem], pid, rid, topo.mask(core, mate[t]))
+        else:
+            tr = [RemoteDMATransfer(dst_ids=[DstId(rid=rid, pnc=pid)], dma_engine_mask=sum(1 << e for e in eng[k * j:k * j + k]),
+                                    remote_sem=far, src=b[0], dst=a[0]) for j, (a, b) in enumerate(pairs)]
+            call = lambda sem: g.remote_dma_fused(tr, local_sem=T.sem[sem])
+        before = [] if nxt["send"] is None else [("q", nxt["send"])]
+        nxt["send"] = issue("G", call, [], [r for a, b in pairs for r in b[1]], (0.0, "i" if before else "first", 1), ("r", more),
+                            s, len(eng), before, up=3.0 if kind in "rs" and t else 0.0)
+        sent["a%s%d" % (kind, t)] = nxt["send"]
+
+    def K(t, lo, hi):
+        return A("kk", 16 * t + lo, 16 * t + hi)
+
+    def lands(t, kind, places):
+        s = "a%s%d" % (kind, t)
+        arrive[s] = len(topo.engines(mate[t], core))
+        for o in places:
+            for name, cols in o[1]:
+                past.setdefault(name, []).append((cols, True, ("a", s), "far"))
+
+    for t in range(3):
+        lands(t, "b", [A("lq%d" % t, 0, 128), A("ls%d" % t, 0, 512)])
+        lands(t, "k", [K(t, 8 - own[t], 16 - own[t])])
+        lands(t, "r", [A("lq%d" % t, 128, 144), A("ls%d" % t, 512, 576)])
+        if t:
+            lands(t, "s", [A("kr", 4 * t, 4 * t + 1)])
+
+    def send_bulk(t):
+        send(t, "b", [(raw(A("lq%d" % t, 0, 128)), raw(A("qb", 128 * t, 128 * t + 128))),
+                      (A("ls%d" % t, 0, 512), A("spl", 128 * t + 128, 128 * t + 640))], 0.8)
+
+    def send_root(t):
+        send(t, "r", [(raw(A("lq%d" % t, 128, 144)), raw(A("qr", 128 * t, 128 * t + 16))),
+                      (A("ls%d" % t, 512, 576), A("sr", 128 * t, 128 * t + 64))], 0.2)
+
+    def send_keys(t):
+        send(t, "k", [(K(t, own[t], own[t] + 8), K(t, own[t], own[t] + 8))], 0.0)
+
+    def send_key(t):
+        send(t, "s", [(A("kr", 4 * t, 4 * t + 1), K(t, own[t], own[t] + 1))], 0.0)
+
+    m_, m8_, p31_, h16_, b15_, z16_ = [A("pf", j, j + 1) for j in range(6)]
+    col = [0, 8, 17]
+
+    def qb(t):
+        return A("qb", 128 * t, 128 * t + 128), A("spl", 512 + 128 * t, 640 + 128 * t)
+
+    def qr(t):
+        return A("qr", 128 * t, 128 * t + 128), A("sr", 128 * t, 128 * t + 128)
+
+    def sp(lo, hi):
+        return A("sp", lo, hi)
+
+    load("Y", A("lw", 16, 32), T.ri[:], 0.3)
+    urgent(50.0)
+    load("S", A("lw", 32, 33), T.ro[:], 0.3)
+    load("S", A("lw", 0, 16), T.le[:], 0.3)
+    load("Y", A("xi"), T.x[:], 1.7)
+    urgent(40.0)
+    load("S", A("ut"), T.u[:], 2.5)
+    load("Y", raw(A("qw")), T.wc[:], 4.0)
+    urgent(20.0)
+    load("Y", A("sw"), T.ws[:], 4.5)
+
+    ms(A("ones"), 1.0)
+    urgent(30.0)
+    iota(A("pi"), [[0, 2], [8, 2]], 0, 1, True)
+    iota(A("ci"), [[1, 16]])
+    iota(A("kper"), [[0, 8], [1, 16]])
+    iota(A("c2"), [[-TB, 2]], TB)
+    run("G", lambda: g.affine_select(T.hot[:], T.ones[:], [[-1, 516]], op_.is_equal, 0.0, 3, 4), [A("hot")], [A("ones")], (0.17, "c", 1032))
+    urgent(20.0)
+    ms(A("sin"), 0.0)
+    fill(A("bt0"), 0.0)
+    ms(A("p32"), 1.0)
+    ms(A("p32", 0, 512, 32), 0.0)
+    fill(A("zb"), 0.0)
+    ts(A("pj", 0, 2), A("pi", 0, 2), 15, op_.bitwise_and)
+    ts(A("pj", 2, 3), A("pi", 2, 3), 31, op_.bitwise_and)
+    ts(A("pj", 3, 4), A("pi", 2, 3), 16, op_.bitwise_and)
+    cp(A("pf", 0, 4), A("pj"))
+    fill(A("p16"), 1.0)
+    fill(A("p16", 0, 128, 16), 0.0)
+    cp(A("bl", 0, 32, 2), A("ci"))
+    cp(A("bl", 1, 32, 2), A("ci"))
+    fill(A("str", 512, 544), 256.0)
+    fill(A("tt", 256, 3 * TB, TB), 256.0)
+    ms(A("sp"), 256)
+    ts(A("mask"), A("kper"), m_, op_.is_equal)
+    ts(A("gl"), A("ci"), 32.0, op_.mult, p31_, op_.add)
+    ts(A("upl"), A("ci", 0, 8), 16.0, op_.mult)
+    for b in range(4):
+        fill(plane(b, 256, 272), 0.0)
+        quant(A("qe", 128 * b, 128 * b + 128), A("spl", 128 * b, 128 * b + 128), A("hot", 3 - b, 515 - b))
+    fill(A("fn", 0, 8), 0.0)
+    act(b15_, m_, act_.Identity, -1.0, 15.0)
+    ts(z16_, m_, 0.0, op_.is_equal, 16.0, op_.mult)
+    ts(A("minl"), A("ci"), b15_, op_.min)
+    ts(A("maxl"), A("ci"), b15_, op_.max)
+    if not all(low):
+        ts(A("inv0"), A("zb"), m_, op_.add, z16_, op_.add)
+    if any(low):
+        ts(A("inv1"), A("zb"), m8_, op_.add, z16_, op_.add)
+    fill(A("pr"), 1.0)
+    fill(A("pr", 15, 241, 15), -1.0)
+    fill(A("pr", 0, 256, 16), 0.0)
+    fill(A("pp"), 1.0)
+    fill(A("pp", 0, 256, 16), 0.0)
+    fill(A("pp", 1, 256, 16), 0.0)
+    fill(A("dif"), -16.0)
+    fill(A("dif", 0, 256, 16), 112.0)
+    fill(A("dif", 7, 256, 16), -32.0)
+    act(A("dif", 15, 256, 16), A("ones", 0, 16), act_.Identity, 240.0, m_)
+    fill(A("rw"), 0.0)
+    fill(A("bt2", 0, 64), 0.0)
+    fill(A("zt1", 0, 128), 0.0)
+    act(A("plc"), A("ci"), act_.Identity, 16.0, m_)
+    for t in range(3):
+        k = 8 + int(t > 0)
+        iota(A("cpa", col[t], col[t] + k), [[1, k]], int(t > 0 and not low[t]))
+        act(A("dum", col[t], col[t] + k), A("plc", 0, k), act_.Identity, 1.0, 256.0)
+    iota(A("c14"), [[-1, 16]], 14)
+    iota(A("pin"), [[0, 256]])
+    iota(A("zt0"), [[0, 512]])
+
+    cp(A("sin", 0, 512, 32), A("lw", 16, 32))
+    ts(A("gt1", 0, 17), A("lw", 16, 33), 496, op_.bitwise_and)
+    act(A("sbl"), ind(A("lw", 0, 16), A("bl")))
+    ts(A("r4", 0, 1), A("lw", 32, 33), 4.0, op_.mult)
+    scan(A("sb"), A("p32"), A("sin", 0, 512))
+    tt(A("gt2", 0, 17), A("gt1", 0, 17), A("lw", 16, 33), op_.add)
+    ts(A("rof", 0, 8, 2), A("ci", 0, 4), A("r4", 0, 1), op_.add)
+    turn(A("str", 0, 512), A("sb"))
+    ts(A("goff", 0, 17), A("gt2", 0, 17), h16_, op_.add)
+    ts(A("sp", 0, 9, 8), A("zb", 0, 2), A("r4", 0, 1), op_.add, 0.25, op_.mult)
+    ts(sp(17, 18), A("r4", 0, 1), 0.25, op_.mult)
+    for b in range(4):
+        act(A("bt0", b, 64, 4), ind(A("xi"), A("rof", 2 * b, 2 * b + 1)))
+    quant(*qr(0), A("bt0"))
+    send_root(0)
+    act(A("tt", 0, 256), ind(A("str"), A("goff", 0, 16)))
+    act(A("tt", TB, TB + 256), ind(A("str"), A("gl")))
+    turn(A("stl"), A("sbl"))
+    act(A("tt", 2 * TB, 2 * TB + 256), ind(A("stl"), A("gl")))
+    for b in range(4):
+        act(plane(b, 0, 256), A("xi", b, 1024, 4), scale=0.5)
+    quant(A("qu"), A("su"), A("ut"))
+    words = ind(A("qu"), A("upl"), True)
+    run("V", lambda: g.vector.tensor_copy(T.qu2[:].bitcast(dt.uint32), words[0]), [A("qu2")], [words], span(words, 1))
+    act(A("su2"), ind(A("su"), A("upl")))
+
+    at = [0]
+
+    def look(parts):
+        a0 = at[0]
+        for win, off in parts:
+            k = 16 * off[2]
+            tt(A("mk", at[0], at[0] + k), ind(win, off), A("mask", 0, k), op_.mult)
+            at[0] += k
+        scan(A("sc", a0, at[0]), A("p16", 0, at[0] - a0), A("mk", a0, at[0]))
+        return a0
+
+    def end(a0, j, k=1):
+        return A("sc", a0 + 16 * j + 15, a0 + 16 * (j + k), 16)
+
+    r2, r21, r213 = A("tt", 0, TB), A("tt", 0, 2 * TB), A("tt", 0, 3 * TB)
+    a = look([(A("str"), A("goff", 16, 17))])
+    cp(sp(1, 2), end(a, 0))
+    ts(A("wo", 2, 3), end(a, 0), 2.0 * TB, op_.add)
+    cp(sp(18, 19), end(a, 0))
+    a = look([(r2, sp(0, 2)), (A("stl"), A("goff", 16, 17))])
+    cp(sp(2, 4), end(a, 0, 2))
+    ts(A("wo", 0, 2), A("c2"), end(a, 2), op_.add)
+    cp(sp(9, 10), end(a, 2))
+    a = look([(r2, sp(2, 4)), (r213, A("wo", 0, 3))])
+    cp(sp(4, 6), end(a, 0, 2))
+    cp(sp(10, 12), end(a, 2, 2))
+    ts(A("wo", 4, 6), A("c2"), end(a, 4), op_.add)
+    cp(sp(19, 20), end(a, 4))
+    a = look([(r2, sp(4, 6)), (r2, sp(10, 12)), (r21, A("wo", 4, 6))])
+    cp(sp(6, 8), end(a, 0, 2))
+    cp(sp(12, 14), end(a, 2, 2))
+    cp(sp(20, 22), end(a, 4, 2))
+    a = look([(r2, sp(12, 14)), (r2, sp(20, 22))])
+    cp(sp(14, 16), end(a, 0, 2))
+    cp(sp(22, 24), end(a, 2, 2))
+    a = look([(r2, sp(22, 23))])
+    cp(sp(24, 25), end(a, 0))
+
+    def spine_tile(t, off, i0, hi, engines):
+        for b in range(4):
+            mul(engines[b], A("bt%d" % t, 64 * i0 + b, 64 * (i0 + off[2]), 4), ind(plane(b, 0, hi), off), 2.0)
+
+    def penalty(lo, hi):
+        ts(A("pen", lo, hi), sp(lo, hi), 256.0, op_.is_equal, -1e29, op_.mult)
+
+    def keys(t, bank):
+        quant(*qb(t), A("bt%d" % t))
+        mm(bank, A("qu2"), A("su2"), *qb(t))
+        km, c = A("km", 128 * t, 128 * t + 128), 128 * t
+        tt(km, A("ps", 512 * bank, 512 * bank + 128), A("mask"), op_.mult)
+        scan(A("ks", c, c + 128), A("p16"), km)
+        tt(K(t, own[t], own[t] + 8), A("ks", c + 15, c + 128, 16), A("pen", col[t], col[t] + 8), op_.add)
+        send_keys(t)
+        send_bulk(t)
+
+    def unpack(q, s):
+        for b in range(4):
+            mm(b, A("qe", 128 * b, 128 * b + 128), A("spl", 128 * b, 128 * b + 128), q, s)
+
+    def fetch(t, c0, c1, to):
+        for b in range(4):
+            act(A("dh%d" % t, 256 * b + to, 256 * b + to + c1 - c0), A("ps", 512 * b + c0, 512 * b + c1), scale=0.5)
+
+    def far(t, c0):
+        return A("lq%d" % t, c0, c0 + 128), A("ls%d" % t, 384 + c0, 512 + c0)
+
+    def places(lo, hi, last):
+        ts(A("e99", lo, hi), sp(lo, hi), 256.0, op_.is_equal, 999.0, op_.mult)
+        ts(A("fn", lo, last), sp(lo + 1, last + 1), 256.0, op_.not_equal)
+        tt(A("pa", lo, hi), A("e99", lo, hi), A("cpa", lo, hi), op_.add)
+        tt(A("pn", lo, hi), A("pa", lo, hi), A("fn", lo, hi), op_.add)
+
+    def positions(t):
+        first = 0.0
+        if not low[t]:
+            first = A("fi", t, t + 1)
+            ts(A("fb", 8 * t, 8 * t + 8), K(t, 0, 8), -5e28, op_.is_gt)
+            red(first, A("fb", 8 * t, 8 * t + 8))
+        for j in range(2):
+            ts(A("pin", 16 * j + 1, 256, 32), A(("pa", "pn")[j], col[t], col[t] + 8), first, op_.add, 15.0, op_.min)
+        scan(A("pe", 256 * t, 256 * t + 256), A("pp"), A("pin"))
+
+    def order(t):
+        for j in range(2):
+            act(A("kx", 128 * j, 128 * j + 128), ind(K(t, 0, 16), A("maxl", 8 * j, 8 * j + 8)))
+        for j in range(2):
+            tt(A("gm", 128 * j, 128 * j + 128), ind(K(t, 0, 16), A("minl", 8 * j, 8 * j + 8)), A("kx", 128 * j, 128 * j + 128), op_.is_ge)
+        scan(A("gs"), A("pr"), A("gm"))
+        tt(A("rw", 0, 16) if t == 0 else A("rk"), A("gs", 15, 256, 16), A("c14"), op_.add)
+
+    def insert(t):
+        s = A("kr", 4 * t, 4 * t + 1)
+        if low[t]:
+            ts(A("bef", 0, 8), K(t, 0, 8), s, op_.is_lt)
+            ts(A("bef", 8, 16), K(t, 8, 16), s, op_.is_le)
+        else:
+            ts(A("bef"), K(t, 0, 16), s, op_.is_le)
+        tt(A("rw", 32 * t, 32 * t + 16), A("rk"), A("bef"), op_.add)
+
+    def lists(t, i0, i1):
+        a0, n0 = (24 * t, 24 * t + 4) if i0 == 0 else (24 * t + 8, 24 * t + 16)
+        return A("off", a0, a0 + i1 - i0), A("off", n0, n0 + i1 - i0)
+
+    def invert(t, i0, i1):
+        lo, hi = 256 * t + 32 * i0, 256 * t + 32 * i1
+        tt(A("nm", lo, hi), ind(A("rw", 32 * t, 32 * t + 32), A("inv%d" % int(low[t]), 0, 2 * (i1 - i0))), A("pe", lo, hi), op_.not_equal)
+        scan(A("iv", lo, hi), A("nm", lo, hi), A("dif", 0, hi - lo))
+        la, ln = lists(t, i0, i1)
+        cp(la, A("iv", lo + 15, hi, 32))
+        cp(ln, A("iv", lo + 31, hi, 32))
+
+    def layer(t, i0, i1, buf, j, bank=4, c=0):
+        n = 16 * (i1 - i0)
+        la, ln = lists(t, i0, i1)
+        q, s = A("qz", 128 * j, 128 * j + 128), A("sz", 128 * j, 128 * j + 128)
+        for b in range(4):
+            act(A(buf, c + n * b, c + n * b + n), ind(A("dh%d" % t, 256 * b, 256 * b + 256), la))
+        for b in range(4):
+            tt(A("zt%d" % j, 64 * i0 + b, 64 * i1, 4), ind(A("dh%d" % t, 256 * b, 256 * b + 256), ln), A(buf, c + n * b, c + n * b + n), op_.add)
+        quant(q, s, A("zt%d" % j))
+        if (t, j) == (2, 0):
+            urgent(1.0)
+        for b in range(4):
+            mm(bank + b, A("qw", 128 * b, 128 * b + 128), A("sw", 128 * b, 128 * b + 128), q, s)
+
+    def relu(eng, o, b, i0, i1, c, bank=4):
+        i = A("ps", 512 * (bank + b) + 16 * i0, 512 * (bank + b) + 16 * i1)
+        if eng == "S":
+            act(o, i, act_.Relu, scale=c)
+        else:
+            ts(o, i, 0.0, op_.max, c, op_.mult)
+
+    def short_road(t):
+        f = FAST[t]
+        n = 16 * f
+        invert(t, 0, f)
+        layer(t, 0, f, "ef", 0)
+        for b in range(4):
+            act(A("ei", b, 4 * n, 4), A("ef", n * b, n * b + n), scale=2.0)
+        for b in range(4):
+            relu("VVSS"[b], A("rf", b, 4 * n, 4), b, 0, f, 0.03125)
+        tt(A("bt%d" % (t + 1), 0, 64), A("rf", 0, 64), A("ei", 0, 64), op_.add)
+        quant(*qr(t + 1), A("bt%d" % (t + 1)))
+        send_root(t + 1)
+        mm(4, A("qu2"), A("su2"), *qr(t + 1))
+        tt(A("kq"), A("ps", 2048, 2064), A("mask", 0, 16), op_.mult)
+        red(K(t + 1, own[t + 1], own[t + 1] + 1), A("kq"))
+        send_key(t + 1)
+
+    def long_road(t):
+        i0, hi = FAST[t], [384, 496][t]
+        n = 16 * (8 - i0)
+        invert(t, i0, 8)
+        layer(t, i0, 8, "eh%d" % t, 1)
+        for b in range(4):
+            relu("S", plane(b, hi - n, hi), b, i0, 8, 0.015625)
+        o = planes(hi - n, hi)
+        dma("G", o[0], T["eh%d" % t][:], o[1], A("eh%d" % t)[1], 1.5, accum_op=op_.add)
+
+    def scatter(lo, hi, v0):
+        o = ind(A("iw"), A("so", lo, hi))
+        i = A("val", v0, v0 + 16 * (hi - lo))
+        run("V", lambda: g.vector.tensor_copy(o[0], i[0]), [A("iw")], [i, A("so", lo, hi)], (0.06, "s", i[2]))
+
+    spine_tile(0, sp(0, 8), 0, 272, "VSVS")
+    penalty(0, 8)
+    keys(0, 4)
+    behind = [("q", nxt["send"])]
+    iota(A("val", 0, 224), [[1, 224]], 288, after=behind)
+    iota(A("val", 224, 240), [[-1, 16]], -512, after=behind)
+    iota(A("val", 240, 336), [[1, 96]], 528, after=behind)
+    iota(A("iw", 0, 256), [[0, 256]], after=behind)
+    iota(A("iw", 256, 512), [[0, 256]], after=behind)
+    unpack(*qb(0))
+    fetch(0, 0, 128, 128)
+    places(0, 8, 7)
+    spine_tile(1, sp(8, 16), 0, 272, "SSSS")
+    penalty(8, 25)
+    ms(A("pen", 8, 18, 9), -3e29)
+    places(8, 25, 25)
+    keys(1, 5)
+    cp(A("ob2", 2, 8), sp(19, 25))
+    ts(A("ot", 0, 1), m_, 16.0, op_.add)
+    ts(A("ot", 1, 2), sp(18, 19), 256.0, op_.not_equal, A("ot", 0, 1), op_.mult)
+    ts(A("ob2", 0, 1), A("ot", 1, 2), 256.0, op_.add)
+    spine_tile(2, A("ob2", 2, 8), 2, 272, "SSSS")
+    unpack(*far(0, 16))
+    positions(0)
+    order(0)
+    fetch(0, 0, 128, 0)
+    unpack(*far(1, 0))
+    short_road(0)
+
+    load("Y", A("vt"), T.v[:], 0.7, A("kq")[1])
+    fetch(1, 16, 128, 0)
+    unpack(*qr(1))
+    fetch(1, 0, 128, 128)
+    tt(A("hr"), A("rf", 64, 128), A("ei", 64, 128), op_.add)
+    for b in range(4):
+        act(plane(b, 272, 288), A("hr", b, 64, 4), scale=0.5)
+    spine_tile(2, A("ob2", 0, 1), 1, 288, "SSSS")
+    keys(2, 5)
+    positions(1)
+    order(1)
+    unpack(*far(1, 16))
+    insert(1)
+    fetch(1, 112, 128, 112)
+    short_road(1)
+
+    f1, f2, f3, f4, f5 = [A("ff", 16 * j, 16 * j + 16) for j in range(5)]
+    cp(A("s1", 0, 25), sp(0, 25))
+    tt(A("s2", 0, 25), A("s1", 0, 25), A("e99", 0, 25), op_.add)
+    tt(A("s3", 0, 25), A("s2", 0, 25), A("dum", 0, 25), op_.min)
+    cp(A("so", 0, 16), A("s3", 0, 16))
+    cp(A("so", 16, 24), A("s3", 17, 25))
+    scatter(2, 8, 0)
+    scatter(8, 16, 80)
+    scatter(16, 24, 208)
+    for h in range(2):
+        dma("Y", T.tw[:, 16 * h:16 * h + 16], T.iw[16 * h::32, :], A("tw", 16 * h, 16 * h + 16)[1], A("iw")[1], 0.5)
+    turn(A("wr"), A("tw"))
+    urgent(6.0)
+    act(f1, A("wr", 0, 16), act_.Abs)
+    tt(f2, f1, A("plc"), op_.max)
+    cp(A("fo"), f2)
+    ts(f3, A("wr", 0, 16), 0.0, op_.is_gt)
+    tt(f4, A("lw", 16, 32), A("lw", 0, 16), op_.subtract)
+    tt(f5, f3, f4, op_.mult)
+    tt(A("ow", 0, 16), A("lw", 0, 16), f5, op_.add)
+    tt(A("ow", 16, 32), A("lw", 16, 32), f5, op_.subtract)
+    turn(A("olt"), A("ow"))
+    for h in range(2):
+        dma("Y", T.ol[h::2, :], T.olt[:, 16 * h:16 * h + 16], ins=A("olt")[1], more=1.0)
+
+    unpack(*qr(2))
+    fetch(2, 0, 128, 128)
+    unpack(*far(2, 0))
+    fetch(2, 16, 128, 0)
+    long_road(0)
+    positions(2)
+    order(2)
+    long_road(1)
+    quant(A("qv"), A("sv"), A("vt"))
+    unpack(*far(2, 16))
+    insert(2)
+    fetch(2, 112, 128, 112)
+    for h in range(2):
+        bank = 4 - 4 * h
+        invert(2, 4 * h, 4 * h + 4)
+        layer(2, 4 * h, 4 * h + 4, "eh2", h, bank, 256 * h)
+        for b in range(4):
+            c = 256 * h + 64 * b
+            relu("S", A("rb", c, c + 64), b, 4 * h, 4 * h + 4, 0.015625, bank)
+            tt(plane(b, 496 + 64 * h, 560 + 64 * h), A("rb", c, c + 64), A("eh2", c, c + 64), op_.add)
+    for h in range(2):
+        c = 128 * h
+        for b in range(4):
+            mul(LAST[h][b], A("xt", 4 * c + b, 4 * c + 512, 4), ind(plane(b, 0, PL), A("fo", 8 * h, 8 * h + 8)), 2.0)
+        q, s = A("qx", c, c + 128), A("sx", c, c + 128)
+        quant(q, s, A("xt", 4 * c, 4 * c + 512))
+        mm(4 + h, A("qv"), A("sv"), q, s)
+        dma("Y", T.oc[:, 4 * c:4 * c + 512], raw(q)[0], ins=q[1], more=0.5)
+        act(A("ys", c, c + 128), A("ps", 512 * (4 + h), 512 * (4 + h) + 128))
+        dma("S", T.y[:, c:c + 128], T.ys[:, c:c + 128], ins=A("ys", c, c + 128)[1], more=0.5)
+    for k in range(4):
+        dma("Y", T.osc[4 * k:4 * k + 4, :], T.sx[32 * k:32 * k + 4, :], ins=A("sx")[1])
+
+    total, direct, token, known, last = dict(arrive), {}, {}, {q: {} for q in queue}, {}
+    for pos, k in enumerate(polish(ops, sent, arrange(ops, sent))):
+        o = ops[k]
+        mine = known[o["eng"]]
+        need = [(d[1], arrive[d[1]], {}, j) if isinstance(d, tuple) else token[d] for j, d in enumerate(sorted(o["deps"], key=str))
+                if not (isinstance(d, tuple) and d[0] == "q")]
+        for s, v, earlier, _ in sorted(need, key=lambda x: -x[3]):
+            if mine.get(s, 0) < v:
+                queue[o["eng"]].wait_ge(T.sem[s], v)
+                direct[s] = max(direct.get(s, 0), v)
+                mine[s] = v
+                for s2, v2 in earlier.items():
+                    mine[s2] = max(mine.get(s2, 0), v2)
+        s = o["sem"] or "c" + o["eng"]
+        total[s] = total.get(s, 0) + o["n"]
+        token[k] = (s, total[s], dict(mine), 1000 + pos)
+        last[s] = pos + (50 if o["lag"] else 0)
+        o["call"](s)
+    for s in sorted(total, key=lambda s: (last.get(s, 0), s)):
+        if direct.get(s, 0) < total[s]:
+            g.wait_ge(T.sem[s], total[s])

@@ -1,12 +1,16 @@
+import numpy as np
 from concourse.bass import DstId, RemoteDMATransfer
 from concourse.mybir import dt, AluOpType, AxisListType, ActivationFunctionType
 
 BF, F32, I32, U16, X4, U8 = "bfloat16", "float32", "int32", "uint16", "float8_e4m3fn_x4", "uint8"
 PL = 624
 TB = 257
+BIG = 2.0 ** 90
 STEP = [1, 2, 4]
 FAST = [2, 1]
 LAST = ["SSSV", "SSVV"]
+B0 = "VSVS"
+RELU = "S"
 PACE = {"c": 0.00104, "g": 0.00162, "s": 0.00395, "p": 0.0006, "wake": 0.07, "l": 2.0, "r": 2.3, "i": 0.5, "first": 2.0, "d": 0.1, "D": 1.0}
 AHEAD = 0.4
 TRIES = 2000
@@ -16,17 +20,18 @@ PACES = [{}, {"c": 0.00083, "g": 0.001, "s": 0.0016, "p": 0.00045, "wake": 0.04,
 
 _S = {
     I32: "lw 36 pi 4 pj 4 gt1 20 gt2 20",
-    U16: "goff 18 bl 32 gl 16 upl 8 minl 16 maxl 16 inv0 16 inv1 16 rof 8 sp 26 wo 8 ob2 8 off 72 so 24 fo 16",
-    F32: "pf 8 ci 16 plc 16 c14 16 c2 2 zb 16 r4 4 cpa 26 dum 26 ot 4 kk 48 kr 12 km 384 ks 384 kq 16 pen 26 e99 26 fn 26 pa 26 pn 26 "
-         "fb 24 fi 4 kx 256 rk 16 bef 16 rf 128 rb 512 val 336 iw 512 s1 26 s2 26 s3 26 tw 32 wr 32 ff 80 ow 32 olt 32 ys 256",
-    BF: "kper 128 mask 128 sin 544 p32 512 p16 128 pp 256 pr 256 dif 256 ones 516 hot 516 sb 512 sbl 512 str 544 stl 512 tt 772 mk 352 sc 352 "
-        "xi 1024 ut 512 vt 512 bt0 512 bt1 512 bt2 512 zt0 512 zt1 512 xt 1024 pin 256 pe 768 gm 256 gs 256 rw 96 nm 768 iv 768 "
-        "dh0 1024 dh1 1024 dh2 1024 ef 128 ei 128 hr 64 eh0 384 eh1 448 eh2 512",
-    X4: "qe 512 qw 512 qb 384 qu 128 qu2 128 qv 128 qr 384 qz 256 qx 256 lq0 144 lq1 144 lq2 144",
-    U8: "sw 512 spl 896 su 128 su2 128 sv 128 sr 384 sz 256 sx 256 ls0 576 ls1 576 ls2 576",
+    U16: "goff 18 bl 32 gl 16 upl 8 minl 16 maxl 16 inv0 16 inv1 16 end0 16 end1 16 rof 8 sp 28 wl 16 ob 2 off 80 so 28 fo 16",
+    F32: "pf 8 ci 16 r4 4 dum 27 kk 72 kr 12 km 384 ks 384 kq 16 pen0 8 cap 48 kx 256 rf 128 rb 512 val 336 iw 512 "
+         "s1 28 s2 27 s3 27 tw 32 wr 32 ff 80 ow 32 olt 32 ys 256 dh0 1024 dh1 1024 dh2 1024 ef 128 ei 64 hr 64 eh0 384 eh1 448 eh2 512",
+    BF: "kper 128 mask 128 sin 544 p32 512 p16 128 pp 256 pr 256 dif 256 ones 516 hot 516 sb 512 sbl 512 str 544 stl 512 tt 785 "
+        "xi 1024 ut 512 vt 512 bt0 512 bt1 512 bt2 512 zf 1120 zt 512 xt 1024 pe 800 gm 256 rw 64 nb 64 pk 32 nm 800 iv 800",
+    X4: "qe 512 qw 512 qb 384 qu 128 qu2 128 qv 128 qr 384 qf 264 qz 256 qx 256 lq0 144 lq1 144 lq2 144",
+    U8: "sw 512 spl 896 su 128 su2 128 sv 128 sr 448 sf 264 sz 256 sx 256 ls0 576 ls1 576 ls2 576",
 }
 SCRATCH = {k: ("sbuf", [128, int(w)], d) for d, s in _S.items() for k, w in zip(s.split()[::2], s.split()[1::2])}
-SCRATCH["xp"] = ("sbuf", [128, 4, PL], F32)
+SCRATCH.update({k: ("sbuf", [128, a, b], d) for k, a, b, d in [
+    ("xp", 4, PL, F32), ("pen", 3, 9, F32), ("fn", 3, 9, F32), ("cpa", 3, 8, F32), ("pq", 3, 16, F32),
+    ("mk", 5, 96, BF), ("sc", 5, 96, BF), ("gs", 3, 272, BF), ("pin", 3, 256, BF)]})
 SCRATCH["ps"] = ("psum", [128, 4096], F32)
 SEMAPHORES = ["cV", "cS", "cP", "cG"] + ["d%d" % i for i in range(28)] + ["l%d" % i for i in range(12)] + \
     ["a%s%d" % (k, t) for k in "bkrs" for t in range(3)]
@@ -155,11 +160,19 @@ def rank_program(g, core, T, topo):
         cols = frozenset([lo // 512]) if name == "ps" else frozenset(range(lo, hi, st))
         return (T[name][:, lo:hi:st], [(name, cols)], len(range(lo, hi, st)), False)
 
-    def plane(b, lo, hi):
-        return (T.xp[:, b, lo:hi], [("xp", frozenset(range(PL * b + lo, PL * b + hi)))], hi - lo, False)
+    def R(name, r, lo=0, hi=None, st=1):
+        w = SCRATCH[name][1][2]
+        hi = w if hi is None else hi
+        rows = range(*r) if isinstance(r, tuple) else [r]
+        cols = frozenset(w * i + c for i in rows for c in range(lo, hi, st))
+        view = T[name][:, r[0]:r[1], lo:hi:st] if isinstance(r, tuple) else T[name][:, r, lo:hi:st]
+        return (view, [(name, cols)], len(cols), False)
 
-    def planes(lo, hi):
-        return (T.xp[:, :, lo:hi], [r for b in range(4) for r in plane(b, lo, hi)[1]], 4 * (hi - lo), False)
+    def plane(b, lo, hi, st=1):
+        return R("xp", b, lo, hi, st)
+
+    def bank(k, lo=0, hi=128, st=1):
+        return A("ps", 512 * k + lo, 512 * k + hi, st)
 
     def ind(win, off, words=False):
         w = win[0].bitcast(dt.uint32) if words else win[0]
@@ -241,13 +254,22 @@ def rank_program(g, core, T, topo):
         else:
             ts(o, i, c, op_.mult)
 
-    def mm(bank, lq, ls, rq, rs):
-        o = A("ps", 512 * bank, 512 * bank + 128)
-        run("P", lambda: g.tensor.matmul_mx(o[0], lq[0], ls[0], rq[0], rs[0], True, True), [o], [lq, ls, rq, rs], (0.0, "p", 144))
+    def mm(k, *sides):
+        o = bank(k)
+
+        def call():
+            for j, (lq, ls, rq, rs) in enumerate(sides):
+                last = g.tensor.matmul_mx(o[0], lq[0], ls[0], rq[0], rs[0], j == 0, j == len(sides) - 1)
+            return last
+        run("P", call, [o], [x for s in sides for x in s], (0.0, "p", 144 * len(sides)))
 
     def iota(o, pat, base=0, ch=0, whole=False, after=()):
         kw = {} if whole else {"allow_small_or_imprecise_dtypes": True}
         run("G", lambda: g.iota(o[0], pat, base, ch, **kw), [o], [], (0.13, "c", 2 * o[2]), after)
+
+    def keep(o, pat, op, base, ch=0, after=()):
+        i = A("ones", 0, o[2])
+        run("G", lambda: g.affine_select(o[0], i[0], pat, op, 0.0, base, ch), [o], [i], (0.17, "c", 2 * o[2]), after)
 
     def dma(eng, out, in_, outs=(), ins=(), more=0.0, quiet=(), **kw):
         s = "d%d" % nxt["d"]
@@ -286,6 +308,9 @@ def rank_program(g, core, T, topo):
     def K(t, lo, hi):
         return A("kk", 16 * t + lo, 16 * t + hi)
 
+    def out_keys(t, lo, hi):
+        return A("kk", 48 + 8 * t + lo, 48 + 8 * t + hi) if low[t] else K(t, 8 + lo, 8 + hi)
+
     def lands(t, kind, places):
         s = "a%s%d" % (kind, t)
         arrive[s] = len(topo.engines(mate[t], core))
@@ -294,28 +319,21 @@ def rank_program(g, core, T, topo):
                 past.setdefault(name, []).append((cols, True, ("a", s), "far"))
 
     for t in range(3):
-        lands(t, "b", [A("lq%d" % t, 0, 128), A("ls%d" % t, 0, 512)])
+        lands(t, "b", [A("lq%d" % t, 16, 128), A("ls%d" % t, 64, 512)])
         lands(t, "k", [K(t, 8 - own[t], 16 - own[t])])
         lands(t, "r", [A("lq%d" % t, 128, 144), A("ls%d" % t, 512, 576)])
         if t:
             lands(t, "s", [A("kr", 4 * t, 4 * t + 1)])
 
     def send_bulk(t):
-        send(t, "b", [(raw(A("lq%d" % t, 0, 128)), raw(A("qb", 128 * t, 128 * t + 128))),
-                      (A("ls%d" % t, 0, 512), A("spl", 128 * t + 128, 128 * t + 640))], 0.8)
+        send(t, "b", [(raw(A("lq%d" % t, 16, 128)), raw(A("qb", 128 * t + 16, 128 * t + 128))),
+                      (A("ls%d" % t, 64, 512), A("spl", 128 * t + 192, 128 * t + 640))], 0.7)
 
     def send_root(t):
-        send(t, "r", [(raw(A("lq%d" % t, 128, 144)), raw(A("qr", 128 * t, 128 * t + 16))),
-                      (A("ls%d" % t, 512, 576), A("sr", 128 * t, 128 * t + 64))], 0.2)
+        c = 128 * t
+        send(t, "r", [(raw(A("lq%d" % t, 128, 144)), raw(A("qr", c, c + 16))), (A("ls%d" % t, 512, 576), A("sr", c, c + 64))], 0.2)
 
-    def send_keys(t):
-        send(t, "k", [(K(t, own[t], own[t] + 8), K(t, own[t], own[t] + 8))], 0.0)
-
-    def send_key(t):
-        send(t, "s", [(A("kr", 4 * t, 4 * t + 1), K(t, own[t], own[t] + 1))], 0.0)
-
-    m_, m8_, p31_, h16_, b15_, z16_ = [A("pf", j, j + 1) for j in range(6)]
-    col = [0, 8, 17]
+    m_, m8_, p31_, h16_, b15_, bm_ = [A("pf", j, j + 1) for j in range(6)]
 
     def qb(t):
         return A("qb", 128 * t, 128 * t + 128), A("spl", 512 + 128 * t, 640 + 128 * t)
@@ -323,8 +341,14 @@ def rank_program(g, core, T, topo):
     def qr(t):
         return A("qr", 128 * t, 128 * t + 128), A("sr", 128 * t, 128 * t + 128)
 
-    def sp(lo, hi):
-        return A("sp", lo, hi)
+    def sp(lo, hi, st=1):
+        return A("sp", lo, hi, st)
+
+    def inv(t, k):
+        return A("inv%d" % int(low[t]), 0, k)
+
+    def ends(t, k):
+        return A("end%d" % int(low[t]), 0, k)
 
     load("Y", A("lw", 16, 32), T.ri[:], 0.3)
     urgent(50.0)
@@ -342,61 +366,59 @@ def rank_program(g, core, T, topo):
     iota(A("pi"), [[0, 2], [8, 2]], 0, 1, True)
     iota(A("ci"), [[1, 16]])
     iota(A("kper"), [[0, 8], [1, 16]])
-    iota(A("c2"), [[-TB, 2]], TB)
-    run("G", lambda: g.affine_select(T.hot[:], T.ones[:], [[-1, 516]], op_.is_equal, 0.0, 3, 4), [A("hot")], [A("ones")], (0.17, "c", 1032))
-    urgent(20.0)
+    keep(A("p16"), [[0, 8], [1, 16]], op_.is_ge, -1)
+    keep(A("hot"), [[-1, 516]], op_.is_equal, 3, 4)
     ms(A("sin"), 0.0)
-    fill(A("bt0"), 0.0)
-    ms(A("p32"), 1.0)
-    ms(A("p32", 0, 512, 32), 0.0)
-    fill(A("zb"), 0.0)
+    fill(A("p32"), 1.0)
+    fill(A("p32", 0, 512, 32), 0.0)
+    ms(A("zf", 64, 608), 0.0)
+    fill(A("zf", 608, 1120), 0.0)
     ts(A("pj", 0, 2), A("pi", 0, 2), 15, op_.bitwise_and)
     ts(A("pj", 2, 3), A("pi", 2, 3), 31, op_.bitwise_and)
     ts(A("pj", 3, 4), A("pi", 2, 3), 16, op_.bitwise_and)
     cp(A("pf", 0, 4), A("pj"))
-    fill(A("p16"), 1.0)
-    fill(A("p16", 0, 128, 16), 0.0)
     cp(A("bl", 0, 32, 2), A("ci"))
     cp(A("bl", 1, 32, 2), A("ci"))
     fill(A("str", 512, 544), 256.0)
-    fill(A("tt", 256, 3 * TB, TB), 256.0)
+    fill(A("tt", 256, 2 * TB, TB), 256.0)
+    fill(A("tt", 784, 785), 256.0)
     ms(A("sp"), 256)
     ts(A("mask"), A("kper"), m_, op_.is_equal)
     ts(A("gl"), A("ci"), 32.0, op_.mult, p31_, op_.add)
     ts(A("upl"), A("ci", 0, 8), 16.0, op_.mult)
+    fill(R("xp", (0, 4), 256, 288), 0.0)
     for b in range(4):
-        fill(plane(b, 256, 272), 0.0)
         quant(A("qe", 128 * b, 128 * b + 128), A("spl", 128 * b, 128 * b + 128), A("hot", 3 - b, 515 - b))
-    fill(A("fn", 0, 8), 0.0)
     act(b15_, m_, act_.Identity, -1.0, 15.0)
-    ts(z16_, m_, 0.0, op_.is_equal, 16.0, op_.mult)
+    act(bm_, m_, act_.Identity, 2.0, 256.0)
     ts(A("minl"), A("ci"), b15_, op_.min)
     ts(A("maxl"), A("ci"), b15_, op_.max)
-    if not all(low):
-        ts(A("inv0"), A("zb"), m_, op_.add, z16_, op_.add)
-    if any(low):
-        ts(A("inv1"), A("zb"), m8_, op_.add, z16_, op_.add)
+    for lo in sorted(set(low)):
+        z_ = A("pf", 6 + lo, 7 + lo)
+        act(z_, A("mask", 0, 1), scale=8.0 if lo else 16.0)
+        ts(A("inv%d" % lo), A("ones", 0, 16), z_, op_.mult, m8_ if lo else m_, op_.add)
+        if lo in low[:2]:
+            ts(A("end%d" % lo), A("inv%d" % lo), 16.0, op_.mult, 15.0, op_.add)
     fill(A("pr"), 1.0)
     fill(A("pr", 15, 241, 15), -1.0)
     fill(A("pr", 0, 256, 16), 0.0)
-    fill(A("pp"), 1.0)
-    fill(A("pp", 0, 256, 16), 0.0)
-    fill(A("pp", 1, 256, 16), 0.0)
     fill(A("dif"), -16.0)
     fill(A("dif", 0, 256, 16), 112.0)
     fill(A("dif", 7, 256, 16), -32.0)
     act(A("dif", 15, 256, 16), A("ones", 0, 16), act_.Identity, 240.0, m_)
-    fill(A("rw"), 0.0)
+    fill(R("gs", (0, 3), 256, 272), 1.0)
+    fill(A("rw"), 1.0)
+    fill(A("nb"), 0.0)
+    fill(R("sc", 1, 15, 16), 0.0)
+    fill(R("sc", 4, 63, 64), 256.0)
+    fill(A("bt1", 0, 64), 0.0)
     fill(A("bt2", 0, 64), 0.0)
-    fill(A("zt1", 0, 128), 0.0)
-    act(A("plc"), A("ci"), act_.Identity, 16.0, m_)
+    fill(A("zt", 0, 128), 0.0)
+    a, b = sorted(out_keys(t, 0, 1)[1][0][1] for t in (1, 2))
+    a, b = sorted([min(a), min(b)])
+    fill(A("kk", a, b + 1, b - a), -3e29)
     for t in range(3):
-        k = 8 + int(t > 0)
-        iota(A("cpa", col[t], col[t] + k), [[1, k]], int(t > 0 and not low[t]))
-        act(A("dum", col[t], col[t] + k), A("plc", 0, k), act_.Identity, 1.0, 256.0)
-    iota(A("c14"), [[-1, 16]], 14)
-    iota(A("pin"), [[0, 256]])
-    iota(A("zt0"), [[0, 512]])
+        fill(A("cap", 16 * t, 16 * t + 16), 10.0 if low[t] else 2.0)
 
     cp(A("sin", 0, 512, 32), A("lw", 16, 32))
     ts(A("gt1", 0, 17), A("lw", 16, 33), 496, op_.bitwise_and)
@@ -407,180 +429,165 @@ def rank_program(g, core, T, topo):
     ts(A("rof", 0, 8, 2), A("ci", 0, 4), A("r4", 0, 1), op_.add)
     turn(A("str", 0, 512), A("sb"))
     ts(A("goff", 0, 17), A("gt2", 0, 17), h16_, op_.add)
-    ts(A("sp", 0, 9, 8), A("zb", 0, 2), A("r4", 0, 1), op_.add, 0.25, op_.mult)
-    ts(sp(17, 18), A("r4", 0, 1), 0.25, op_.mult)
+    ts(sp(0, 19, 18), A("ones", 0, 2), A("r4", 0, 1), op_.mult, 0.25, op_.mult)
     for b in range(4):
-        act(A("bt0", b, 64, 4), ind(A("xi"), A("rof", 2 * b, 2 * b + 1)))
-    quant(*qr(0), A("bt0"))
+        act(A("zf", b, 64, 4), ind(A("xi"), A("rof", 2 * b, 2 * b + 1)))
+    quant(*qr(0), A("zf", 0, 512))
     send_root(0)
+    behind = [("q", nxt["send"])]
     act(A("tt", 0, 256), ind(A("str"), A("goff", 0, 16)))
-    act(A("tt", TB, TB + 256), ind(A("str"), A("gl")))
     turn(A("stl"), A("sbl"))
-    act(A("tt", 2 * TB, 2 * TB + 256), ind(A("stl"), A("gl")))
+    act(A("tt", 528, 784), ind(A("stl"), A("gl")))
+    act(A("tt", TB, TB + 256), ind(A("str"), A("gl")))
     for b in range(4):
         act(plane(b, 0, 256), A("xi", b, 1024, 4), scale=0.5)
     quant(A("qu"), A("su"), A("ut"))
     words = ind(A("qu"), A("upl"), True)
     run("V", lambda: g.vector.tensor_copy(T.qu2[:].bitcast(dt.uint32), words[0]), [A("qu2")], [words], span(words, 1))
     act(A("su2"), ind(A("su"), A("upl")))
+    keep(A("pp"), [[0, 16], [1, 16]], op_.is_ge, -2)
+    iota(R("cpa", (0, 3)), [[0, 3], [1, 8]], -5)
+    for t in range(3):
+        iota(R("pin", t), [[0, 256]], 1, after=behind)
+        if low[t]:
+            fill(R("pin", t, 8, 256, 16), -15.0)
 
-    at = [0]
+    def look(row, parts):
+        for j, win, off in parts:
+            tt(R("mk", row, 16 * j, 16 * (j + off[2])), ind(win, off), A("mask", 0, 16 * off[2]), op_.mult)
+        lo, hi = 16 * parts[0][0], 16 * (parts[-1][0] + parts[-1][2][2])
+        scan(R("sc", row, lo, hi), A("p16", 0, hi - lo), R("mk", row, lo, hi))
 
-    def look(parts):
-        a0 = at[0]
-        for win, off in parts:
-            k = 16 * off[2]
-            tt(A("mk", at[0], at[0] + k), ind(win, off), A("mask", 0, k), op_.mult)
-            at[0] += k
-        scan(A("sc", a0, at[0]), A("p16", 0, at[0] - a0), A("mk", a0, at[0]))
-        return a0
+    def end(row, j0, j1, st=1):
+        return R("sc", row, 16 * j0 + 15, 16 * j1, 16 * st)
 
-    def end(a0, j, k=1):
-        return A("sc", a0 + 16 * j + 15, a0 + 16 * (j + k), 16)
-
-    r2, r21, r213 = A("tt", 0, TB), A("tt", 0, 2 * TB), A("tt", 0, 3 * TB)
-    a = look([(A("str"), A("goff", 16, 17))])
-    cp(sp(1, 2), end(a, 0))
-    ts(A("wo", 2, 3), end(a, 0), 2.0 * TB, op_.add)
-    cp(sp(18, 19), end(a, 0))
-    a = look([(r2, sp(0, 2)), (A("stl"), A("goff", 16, 17))])
-    cp(sp(2, 4), end(a, 0, 2))
-    ts(A("wo", 0, 2), A("c2"), end(a, 2), op_.add)
-    cp(sp(9, 10), end(a, 2))
-    a = look([(r2, sp(2, 4)), (r213, A("wo", 0, 3))])
-    cp(sp(4, 6), end(a, 0, 2))
-    cp(sp(10, 12), end(a, 2, 2))
-    ts(A("wo", 4, 6), A("c2"), end(a, 4), op_.add)
-    cp(sp(19, 20), end(a, 4))
-    a = look([(r2, sp(4, 6)), (r2, sp(10, 12)), (r21, A("wo", 4, 6))])
-    cp(sp(6, 8), end(a, 0, 2))
-    cp(sp(12, 14), end(a, 2, 2))
-    cp(sp(20, 22), end(a, 4, 2))
-    a = look([(r2, sp(12, 14)), (r2, sp(20, 22))])
-    cp(sp(14, 16), end(a, 0, 2))
-    cp(sp(22, 24), end(a, 2, 2))
-    a = look([(r2, sp(22, 23))])
-    cp(sp(24, 25), end(a, 0))
+    r2, r21, left = A("tt", 0, TB), A("tt", 0, 2 * TB), A("tt", 528, 785)
+    look(1, [(1, A("str"), A("goff", 16, 17))])
+    cp(sp(1, 2), end(1, 1, 2))
+    look(0, [(0, r2, sp(0, 2))])
+    cp(sp(2, 4), end(0, 0, 2))
+    look(1, [(2, left, sp(0, 2)), (4, r2, sp(2, 4))])
+    cp(A("wl", 2, 6), end(1, 2, 6))
+    ts(A("wl", 0, 2), end(1, 2, 4), float(TB), op_.add)
+    look(2, [(0, r21, A("wl", 0, 6))])
+    cp(sp(4, 8), end((1, 3), 4, 6))
+    cp(A("wl", 6, 10), end(2, 0, 4))
+    look(3, [(0, r2, A("wl", 6, 10))])
+    cp(A("wl", 10, 13), end(3, 0, 3))
+    look(4, [(0, r2, A("wl", 10, 13))])
+    cp(sp(9, 17), end((1, 5), 0, 3, 2))
+    cp(sp(19, 27), end((1, 5), 1, 4, 2))
 
     def spine_tile(t, off, i0, hi, engines):
         for b in range(4):
             mul(engines[b], A("bt%d" % t, 64 * i0 + b, 64 * (i0 + off[2]), 4), ind(plane(b, 0, hi), off), 2.0)
 
-    def penalty(lo, hi):
-        ts(A("pen", lo, hi), sp(lo, hi), 256.0, op_.is_equal, -1e29, op_.mult)
-
-    def keys(t, bank):
+    def keys(t, pen):
+        i0, c = int(t > 0), 128 * t
         quant(*qb(t), A("bt%d" % t))
-        mm(bank, A("qu2"), A("su2"), *qb(t))
-        km, c = A("km", 128 * t, 128 * t + 128), 128 * t
-        tt(km, A("ps", 512 * bank, 512 * bank + 128), A("mask"), op_.mult)
-        scan(A("ks", c, c + 128), A("p16"), km)
-        tt(K(t, own[t], own[t] + 8), A("ks", c + 15, c + 128, 16), A("pen", col[t], col[t] + 8), op_.add)
-        send_keys(t)
+        mm(6, (A("qu2"), A("su2"), *qb(t)))
+        km, ks = A("km", c + 16 * i0, c + 128), A("ks", c + 16 * i0, c + 128)
+        tt(km, bank(6, 16 * i0, 128), A("mask", 16 * i0, 128), op_.mult)
+        scan(ks, A("p16", 16 * i0, 128), km)
+        s = A("ks", c + 16 * i0 + 15, c + 128, 16)
+        tt(out_keys(t, i0, 8), s, pen, op_.add if low[t] else op_.subtract)
+        send(t, "k", [(K(t, own[t], own[t] + 8), out_keys(t, 0, 8))], 0.0)
+        if low[t]:
+            tt(K(t, i0, 8), s, pen, op_.subtract)
         send_bulk(t)
 
-    def unpack(q, s):
+    def unpack(t, q, s, to):
         for b in range(4):
-            mm(b, A("qe", 128 * b, 128 * b + 128), A("spl", 128 * b, 128 * b + 128), q, s)
-
-    def fetch(t, c0, c1, to):
+            mm(b, (A("qe", 128 * b, 128 * b + 128), A("spl", 128 * b, 128 * b + 128), q, s))
         for b in range(4):
-            act(A("dh%d" % t, 256 * b + to, 256 * b + to + c1 - c0), A("ps", 512 * b + c0, 512 * b + c1), scale=0.5)
+            act(A("dh%d" % t, 256 * b + to, 256 * b + to + 128), bank(b), scale=0.5)
 
-    def far(t, c0):
-        return A("lq%d" % t, c0, c0 + 128), A("ls%d" % t, 384 + c0, 512 + c0)
-
-    def places(lo, hi, last):
-        ts(A("e99", lo, hi), sp(lo, hi), 256.0, op_.is_equal, 999.0, op_.mult)
-        ts(A("fn", lo, last), sp(lo + 1, last + 1), 256.0, op_.not_equal)
-        tt(A("pa", lo, hi), A("e99", lo, hi), A("cpa", lo, hi), op_.add)
-        tt(A("pn", lo, hi), A("pa", lo, hi), A("fn", lo, hi), op_.add)
-
-    def positions(t):
-        first = 0.0
-        if not low[t]:
-            first = A("fi", t, t + 1)
-            ts(A("fb", 8 * t, 8 * t + 8), K(t, 0, 8), -5e28, op_.is_gt)
-            red(first, A("fb", 8 * t, 8 * t + 8))
-        for j in range(2):
-            ts(A("pin", 16 * j + 1, 256, 32), A(("pa", "pn")[j], col[t], col[t] + 8), first, op_.add, 15.0, op_.min)
-        scan(A("pe", 256 * t, 256 * t + 256), A("pp"), A("pin"))
+    def far(t):
+        return A("lq%d" % t, 16, 144), A("ls%d" % t, 400, 528)
 
     def order(t):
         for j in range(2):
             act(A("kx", 128 * j, 128 * j + 128), ind(K(t, 0, 16), A("maxl", 8 * j, 8 * j + 8)))
         for j in range(2):
             tt(A("gm", 128 * j, 128 * j + 128), ind(K(t, 0, 16), A("minl", 8 * j, 8 * j + 8)), A("kx", 128 * j, 128 * j + 128), op_.is_ge)
-        scan(A("gs"), A("pr"), A("gm"))
-        tt(A("rw", 0, 16) if t == 0 else A("rk"), A("gs", 15, 256, 16), A("c14"), op_.add)
+        scan(R("gs", t, 0, 256), A("pr"), A("gm"))
 
     def insert(t):
-        s = A("kr", 4 * t, 4 * t + 1)
+        s, c = A("kr", 4 * t, 4 * t + 1), 32 * t - 32
         if low[t]:
-            ts(A("bef", 0, 8), K(t, 0, 8), s, op_.is_lt)
-            ts(A("bef", 8, 16), K(t, 8, 16), s, op_.is_le)
+            ts(A("nb", c, c + 8), K(t, 0, 8), s, op_.is_lt, -1.0, op_.mult)
+            ts(A("nb", c + 8, c + 16), K(t, 8, 16), s, op_.is_le, -1.0, op_.mult)
         else:
-            ts(A("bef"), K(t, 0, 16), s, op_.is_le)
-        tt(A("rw", 32 * t, 32 * t + 16), A("rk"), A("bef"), op_.add)
+            ts(A("nb", c, c + 16), K(t, 0, 16), s, op_.is_le, -1.0, op_.mult)
 
-    def lists(t, i0, i1):
-        a0, n0 = (24 * t, 24 * t + 4) if i0 == 0 else (24 * t + 8, 24 * t + 16)
-        return A("off", a0, a0 + i1 - i0), A("off", n0, n0 + i1 - i0)
+    def ranks(t):
+        c = 32 * t - 32
+        tt(A("rw", c, c + 16), R("gs", t, 15, 256, 16), A("nb", c, c + 16), op_.subtract)
+        return A("rw", c, c + 32)
 
-    def invert(t, i0, i1):
-        lo, hi = 256 * t + 32 * i0, 256 * t + 32 * i1
-        tt(A("nm", lo, hi), ind(A("rw", 32 * t, 32 * t + 32), A("inv%d" % int(low[t]), 0, 2 * (i1 - i0))), A("pe", lo, hi), op_.not_equal)
-        scan(A("iv", lo, hi), A("nm", lo, hi), A("dif", 0, hi - lo))
-        la, ln = lists(t, i0, i1)
-        cp(la, A("iv", lo + 15, hi, 32))
-        cp(ln, A("iv", lo + 31, hi, 32))
+    at = [0]
 
-    def layer(t, i0, i1, buf, j, bank=4, c=0):
-        n = 16 * (i1 - i0)
-        la, ln = lists(t, i0, i1)
+    def invert(have, wants, out):
+        lo = at[0]
+        for want in wants:
+            tt(A("nm", at[0], at[0] + want[2]), have, want, op_.not_equal)
+            at[0] += want[2]
+        scan(A("iv", lo, at[0]), A("nm", lo, at[0]), A("dif", 0, at[0] - lo))
+        cp(out, A("iv", lo + 15, at[0], 16))
+
+    def wanted(t, i0, i1):
+        return [A("pe", 256 * t + c + 16 * i0, 256 * t + c + 16 * i1) for c in (0, 128)]
+
+    def window(t, b):
+        return A("dh%d" % t, 256 * b, 256 * b + 256)
+
+    def layer(t, i0, la, ln, buf, c, tile, j, k0):
+        n = 16 * la[2]
         q, s = A("qz", 128 * j, 128 * j + 128), A("sz", 128 * j, 128 * j + 128)
         for b in range(4):
-            act(A(buf, c + n * b, c + n * b + n), ind(A("dh%d" % t, 256 * b, 256 * b + 256), la))
+            act(A(buf, c + n * b, c + n * b + n), ind(window(t, b), la))
         for b in range(4):
-            tt(A("zt%d" % j, 64 * i0 + b, 64 * i1, 4), ind(A("dh%d" % t, 256 * b, 256 * b + 256), ln), A(buf, c + n * b, c + n * b + n), op_.add)
-        quant(q, s, A("zt%d" % j))
-        if (t, j) == (2, 0):
-            urgent(1.0)
+            tt(A(tile, 64 * i0 + b, 64 * i0 + 4 * n, 4), ind(window(t, b), ln), A(buf, c + n * b, c + n * b + n), op_.add)
+        quant(q, s, A(tile, 0, 512))
         for b in range(4):
-            mm(bank + b, A("qw", 128 * b, 128 * b + 128), A("sw", 128 * b, 128 * b + 128), q, s)
+            mm(k0 + b, (A("qw", 128 * b, 128 * b + 128), A("sw", 128 * b, 128 * b + 128), q, s))
 
-    def relu(eng, o, b, i0, i1, c, bank=4):
-        i = A("ps", 512 * (bank + b) + 16 * i0, 512 * (bank + b) + 16 * i1)
+    def relu(eng, o, i, c):
         if eng == "S":
             act(o, i, act_.Relu, scale=c)
         else:
             ts(o, i, 0.0, op_.max, c, op_.mult)
 
-    def short_road(t):
-        f = FAST[t]
-        n = 16 * f
-        invert(t, 0, f)
-        layer(t, 0, f, "ef", 0)
+    def short_road(t, la, ln):
+        n = 16 * la[2]
+        w = 8 * n + 8
         for b in range(4):
-            act(A("ei", b, 4 * n, 4), A("ef", n * b, n * b + n), scale=2.0)
+            act(A("ef", b, 4 * n, 4), ind(window(t, b), la))
         for b in range(4):
-            relu("VVSS"[b], A("rf", b, 4 * n, 4), b, 0, f, 0.03125)
-        tt(A("bt%d" % (t + 1), 0, 64), A("rf", 0, 64), A("ei", 0, 64), op_.add)
+            tt(A("zf", 88 + b, 64 + 32 * n, 32), ind(window(t, b), ln), A("ef", b, 4 * n, 4), op_.add)
+        act(A("ei"), A("ef", 0, 64), scale=2.0)
+        quant(A("qf", 0, w), A("sf", 0, w), A("zf", 64, 64 + 4 * w))
+        for i in range(la[2]):
+            c = [128 * i + 6 - 2 * b for b in range(4)]
+            mm(4 + i, *[(A("qw", 128 * b, 128 * b + 128), A("sw", 128 * b, 128 * b + 128), A("qf", c[b], c[b] + 128), A("sf", c[b], c[b] + 128))
+                        for b in range(4)])
+        relu(RELU, A("rf", 0, 64), bank(4, 0, 128, 2), 0.03125)
+        tt(A("bt%d" % (t + 1), 0, 64), A("rf", 0, 64), A("ei"), op_.add)
         quant(*qr(t + 1), A("bt%d" % (t + 1)))
         send_root(t + 1)
-        mm(4, A("qu2"), A("su2"), *qr(t + 1))
-        tt(A("kq"), A("ps", 2048, 2064), A("mask", 0, 16), op_.mult)
-        red(K(t + 1, own[t + 1], own[t + 1] + 1), A("kq"))
-        send_key(t + 1)
+        mm(7, (A("qu2"), A("su2"), *qr(t + 1)))
+        tt(A("kq"), bank(7, 0, 16), A("mask", 0, 16), op_.mult)
+        mine = K(t + 1, own[t + 1], own[t + 1] + 1)
+        red(mine, A("kq"))
+        send(t + 1, "s", [(A("kr", 4 * t + 4, 4 * t + 5), mine)], 0.0)
 
-    def long_road(t):
+    def long_road(t, la, ln, k0):
         i0, hi = FAST[t], [384, 496][t]
         n = 16 * (8 - i0)
-        invert(t, i0, 8)
-        layer(t, i0, 8, "eh%d" % t, 1)
+        layer(t, i0, la, ln, "eh%d" % t, 0, "zt", 1, k0)
         for b in range(4):
-            relu("S", plane(b, hi - n, hi), b, i0, 8, 0.015625)
-        o = planes(hi - n, hi)
+            relu("S", plane(b, hi - n, hi), bank(k0 + b, 128 - n, 128), 0.015625)
+        o = R("xp", (0, 4), hi - n, hi)
         dma("G", o[0], T["eh%d" % t][:], o[1], A("eh%d" % t)[1], 1.5, accum_op=op_.add)
 
     def scatter(lo, hi, v0):
@@ -588,68 +595,69 @@ def rank_program(g, core, T, topo):
         i = A("val", v0, v0 + 16 * (hi - lo))
         run("V", lambda: g.vector.tensor_copy(o[0], i[0]), [A("iw")], [i, A("so", lo, hi)], (0.06, "s", i[2]))
 
-    spine_tile(0, sp(0, 8), 0, 272, "VSVS")
-    penalty(0, 8)
-    keys(0, 4)
+    def off(lo, hi, st=1):
+        return A("off", lo, hi, st)
+
+    spine_tile(0, sp(0, 8), 0, 272, B0)
+    ts(A("pen0"), sp(0, 8), 256.0, op_.is_equal, BIG, op_.mult)
+    keys(0, A("pen0"))
     behind = [("q", nxt["send"])]
-    iota(A("val", 0, 224), [[1, 224]], 288, after=behind)
-    iota(A("val", 224, 240), [[-1, 16]], -512, after=behind)
+    iota(A("val", 0, 16), [[1, 16]], 496, after=behind)
+    iota(A("val", 16, 32), [[-1, 16]], -512, after=behind)
+    iota(A("val", 32, 240), [[1, 208]], 288, after=behind)
     iota(A("val", 240, 336), [[1, 96]], 528, after=behind)
-    iota(A("iw", 0, 256), [[0, 256]], after=behind)
+    iota(A("iw", 0, 256), [[1, 256]], after=behind)
     iota(A("iw", 256, 512), [[0, 256]], after=behind)
-    unpack(*qb(0))
-    fetch(0, 0, 128, 128)
-    places(0, 8, 7)
-    spine_tile(1, sp(8, 16), 0, 272, "SSSS")
-    penalty(8, 25)
-    ms(A("pen", 8, 18, 9), -3e29)
-    places(8, 25, 25)
-    keys(1, 5)
-    cp(A("ob2", 2, 8), sp(19, 25))
-    ts(A("ot", 0, 1), m_, 16.0, op_.add)
-    ts(A("ot", 1, 2), sp(18, 19), 256.0, op_.not_equal, A("ot", 0, 1), op_.mult)
-    ts(A("ob2", 0, 1), A("ot", 1, 2), 256.0, op_.add)
-    spine_tile(2, A("ob2", 2, 8), 2, 272, "SSSS")
-    unpack(*far(0, 16))
-    positions(0)
+    iota(A("s3"), [[0, 3], [16, 9]], 256, after=behind)
+    act(A("dum"), A("s3"), act_.Identity, 1.0, m_)
+    unpack(0, *qb(0), 128)
+    cp(A("s1"), sp(0, 28))
+    act(R("pen", (0, 3)), A("s1", 0, 27), act_.Relu, BIG, -255.0 * BIG)
+    act(R("fn", (0, 3)), A("s1", 1, 28), act_.Sign, -1.0, 256.0)
+    tt(R("pq", (0, 3), 0, 8), R("pen", (0, 3), 0, 8), R("cpa", (0, 3)), op_.add)
+    tt(R("pq", (0, 3), 8, 16), R("pq", (0, 3), 0, 8), R("fn", (0, 3), 0, 8), op_.add)
+    tt(R("pin", (0, 3), 1, 256, 16), R("pq", (0, 3)), A("cap"), op_.min)
+    for t in range(3):
+        scan(A("pe", 256 * t, 256 * t + 256), A("pp"), R("pin", t))
+    spine_tile(1, sp(10, 17), 1, 272, "SSSS")
+    keys(1, R("pen", 1, 1, 8))
+    ts(A("ob", 0, 1), sp(1, 2), 256.0, op_.not_equal, bm_, op_.add)
+    spine_tile(2, sp(20, 26), 2, 272, "SSSS")
     order(0)
-    fetch(0, 0, 128, 0)
-    unpack(*far(1, 0))
-    short_road(0)
+    unpack(0, *far(0), 0)
+    invert(ind(R("gs", 0), ends(0, 2)), wanted(0, 0, 2), off(0, 4))
+    short_road(0, off(0, 2), off(2, 4))
 
     load("Y", A("vt"), T.v[:], 0.7, A("kq")[1])
-    fetch(1, 16, 128, 0)
-    unpack(*qr(1))
-    fetch(1, 0, 128, 128)
-    tt(A("hr"), A("rf", 64, 128), A("ei", 64, 128), op_.add)
+    unpack(1, *qr(1), 128)
+    relu("S", A("rf", 64, 128), bank(5, 0, 128, 2), 0.015625)
+    tt(A("hr"), A("rf", 64, 128), A("ef", 64, 128), op_.add)
     for b in range(4):
-        act(plane(b, 272, 288), A("hr", b, 64, 4), scale=0.5)
-    spine_tile(2, A("ob2", 0, 1), 1, 288, "SSSS")
-    keys(2, 5)
-    positions(1)
+        act(plane(b, 257, 288, 2), A("hr", b, 64, 4))
+    spine_tile(2, A("ob", 0, 1), 1, 288, "SSSS")
+    keys(2, R("pen", 2, 1, 8))
     order(1)
-    unpack(*far(1, 16))
+    for j, want in enumerate(wanted(1, 0, 1)):
+        tt(A("pk", 16 * j, 16 * j + 16), ind(R("gs", 1), ends(1, 1)), want, op_.subtract)
+    unpack(1, *far(1), 0)
     insert(1)
-    fetch(1, 112, 128, 112)
-    short_road(1)
+    invert(ind(A("nb", 0, 32), inv(1, 2)), [A("pk")], off(4, 8, 2))
+    short_road(1, off(4, 5), off(6, 7))
 
-    f1, f2, f3, f4, f5 = [A("ff", 16 * j, 16 * j + 16) for j in range(5)]
-    cp(A("s1", 0, 25), sp(0, 25))
-    tt(A("s2", 0, 25), A("s1", 0, 25), A("e99", 0, 25), op_.add)
-    tt(A("s3", 0, 25), A("s2", 0, 25), A("dum", 0, 25), op_.min)
-    cp(A("so", 0, 16), A("s3", 0, 16))
-    cp(A("so", 16, 24), A("s3", 17, 25))
-    scatter(2, 8, 0)
-    scatter(8, 16, 80)
-    scatter(16, 24, 208)
+    f1, f3, f4, f5 = [A("ff", 16 * j, 16 * j + 16) for j in range(4)]
+    tt(A("s2"), A("s1", 0, 27), R("pen", (0, 3)), op_.add)
+    tt(A("s3"), A("s2"), A("dum"), op_.min)
+    cp(A("so", 0, 27), A("s3"))
+    scatter(0, 8, 0)
+    scatter(10, 17, 128)
+    scatter(20, 26, 240)
     for h in range(2):
         dma("Y", T.tw[:, 16 * h:16 * h + 16], T.iw[16 * h::32, :], A("tw", 16 * h, 16 * h + 16)[1], A("iw")[1], 0.5)
     turn(A("wr"), A("tw"))
     urgent(6.0)
     act(f1, A("wr", 0, 16), act_.Abs)
-    tt(f2, f1, A("plc"), op_.max)
-    cp(A("fo"), f2)
-    ts(f3, A("wr", 0, 16), 0.0, op_.is_gt)
+    cp(A("fo"), f1)
+    ts(f3, A("wr", 0, 16), 288.0, op_.is_ge)
     tt(f4, A("lw", 16, 32), A("lw", 0, 16), op_.subtract)
     tt(f5, f3, f4, op_.mult)
     tt(A("ow", 0, 16), A("lw", 0, 16), f5, op_.add)
@@ -658,25 +666,23 @@ def rank_program(g, core, T, topo):
     for h in range(2):
         dma("Y", T.ol[h::2, :], T.olt[:, 16 * h:16 * h + 16], ins=A("olt")[1], more=1.0)
 
-    unpack(*qr(2))
-    fetch(2, 0, 128, 128)
-    unpack(*far(2, 0))
-    fetch(2, 16, 128, 0)
-    long_road(0)
-    positions(2)
+    invert(ind(R("gs", 0), ends(0, 6)), wanted(0, 2, 8), off(8, 20))
+    long_road(0, off(8, 14), off(14, 20), 0)
+    unpack(2, *qr(2), 128)
     order(2)
-    long_road(1)
+    invert(ind(ranks(1), inv(1, 16)), [A("pe", 256, 512)], off(21, 37))
+    long_road(1, off(22, 29), off(30, 37), 4)
     quant(A("qv"), A("sv"), A("vt"))
-    unpack(*far(2, 16))
+    unpack(2, *far(2), 0)
     insert(2)
-    fetch(2, 112, 128, 112)
+    rw = ranks(2)
     for h in range(2):
-        bank = 4 - 4 * h
-        invert(2, 4 * h, 4 * h + 4)
-        layer(2, 4 * h, 4 * h + 4, "eh2", h, bank, 256 * h)
+        k0, c = 4 - 4 * h, 40 + 8 * h
+        invert(ind(rw, inv(2, 4)), wanted(2, 4 * h, 4 * h + 4), off(c, c + 8))
+        layer(2, 4 * h, off(c, c + 4), off(c + 4, c + 8), "eh2", 256 * h, ["zf", "zt"][h], h, k0)
         for b in range(4):
             c = 256 * h + 64 * b
-            relu("S", A("rb", c, c + 64), b, 4 * h, 4 * h + 4, 0.015625, bank)
+            relu("S", A("rb", c, c + 64), bank(k0 + b, 64 * h, 64 * h + 64), 0.015625)
             tt(plane(b, 496 + 64 * h, 560 + 64 * h), A("rb", c, c + 64), A("eh2", c, c + 64), op_.add)
     for h in range(2):
         c = 128 * h
@@ -684,9 +690,9 @@ def rank_program(g, core, T, topo):
             mul(LAST[h][b], A("xt", 4 * c + b, 4 * c + 512, 4), ind(plane(b, 0, PL), A("fo", 8 * h, 8 * h + 8)), 2.0)
         q, s = A("qx", c, c + 128), A("sx", c, c + 128)
         quant(q, s, A("xt", 4 * c, 4 * c + 512))
-        mm(4 + h, A("qv"), A("sv"), q, s)
+        mm(4 + h, (A("qv"), A("sv"), q, s))
         dma("Y", T.oc[:, 4 * c:4 * c + 512], raw(q)[0], ins=q[1], more=0.5)
-        act(A("ys", c, c + 128), A("ps", 512 * (4 + h), 512 * (4 + h) + 128))
+        act(A("ys", c, c + 128), bank(4 + h))
         dma("S", T.y[:, c:c + 128], T.ys[:, c:c + 128], ins=A("ys", c, c + 128)[1], more=0.5)
     for k in range(4):
         dma("Y", T.osc[4 * k:4 * k + 4, :], T.sx[32 * k:32 * k + 4, :], ins=A("sx")[1])

@@ -1,39 +1,41 @@
-import numpy as np
 from concourse.bass import DstId, RemoteDMATransfer
 from concourse.mybir import dt, AluOpType, AxisListType, ActivationFunctionType
 
 BF, F32, I32, U16, X4, U8 = "bfloat16", "float32", "int32", "uint16", "float8_e4m3fn_x4", "uint8"
-PL = 624
-TB = 257
+PL = 608
+TB = 272
 BIG = 2.0 ** 90
 STEP = [1, 2, 4]
 FAST = [2, 1]
 LAST = ["SSSV", "SSVV"]
 B0 = "VSVS"
 RELU = "S"
-PACE = {"c": 0.00104, "g": 0.00162, "s": 0.00395, "p": 0.0006, "wake": 0.07, "l": 2.0, "r": 2.3, "i": 0.5, "first": 2.0, "d": 0.1, "D": 1.0}
+PATCH = False
+ADD = "GV"
+UP0 = 1.5
+PACE = {"c": 0.00105, "g": 0.0015, "s": 0.0035, "p": 0.0006, "wake": 0.14, "l": 1.3, "r": 1.4, "i": 0.4, "first": 2.0, "d": 0.1, "D": 1.0}
 AHEAD = 0.4
 TRIES = 2000
-PACES = [{}, {"c": 0.00083, "g": 0.001, "s": 0.0016, "p": 0.00045, "wake": 0.04, "l": 1.7, "r": 1.5, "i": 0.3, "first": 1.0},
-         {"c": 0.00124, "g": 0.0024, "s": 0.0065, "p": 0.0009, "wake": 0.1}, {"r": 3.2, "i": 1.0, "first": 3.0, "l": 2.4, "D": 1.5},
-         {"wake": 0.15, "d": 0.3, "l": 2.3}]
+PACES = [{}, {"c": 0.0009, "g": 0.001, "s": 0.0016, "p": 0.00045, "wake": 0.08, "l": 1.0, "r": 1.0, "i": 0.3, "first": 1.5},
+         {"c": 0.0014, "g": 0.0024, "s": 0.0065, "p": 0.0009}, {"r": 2.6, "i": 0.8, "first": 3.0, "l": 2.0, "D": 1.5},
+         {"wake": 0.2, "d": 0.2}]
 
 _S = {
     I32: "lw 36 pi 4 pj 4 gt1 20 gt2 20",
-    U16: "goff 18 bl 32 gl 16 upl 8 minl 16 maxl 16 inv0 16 inv1 16 end0 16 end1 16 rof 8 sp 28 wl 16 ob 2 off 80 so 28 fo 16",
-    F32: "pf 8 ci 16 r4 4 dum 27 kk 72 kr 12 km 384 ks 384 kq 16 pen0 8 cap 48 kx 256 rf 128 rb 512 val 336 iw 512 "
-         "s1 28 s2 27 s3 27 tw 32 wr 32 ff 80 ow 32 olt 32 ys 256 dh0 1024 dh1 1024 dh2 1024 ef 128 ei 64 hr 64 eh0 384 eh1 448 eh2 512",
-    BF: "kper 128 mask 128 sin 544 p32 512 p16 128 pp 256 pr 256 dif 256 ones 516 hot 516 sb 512 sbl 512 str 544 stl 512 tt 785 "
-        "xi 1024 ut 512 vt 512 bt0 512 bt1 512 bt2 512 zf 1120 zt 512 xt 1024 pe 800 gm 256 rw 64 nb 64 pk 32 nm 800 iv 800",
-    X4: "qe 512 qw 512 qb 384 qu 128 qu2 128 qv 128 qr 384 qf 264 qz 256 qx 256 lq0 144 lq1 144 lq2 144",
-    U8: "sw 512 spl 896 su 128 su2 128 sv 128 sr 448 sf 264 sz 256 sx 256 ls0 576 ls1 576 ls2 576",
+    U16: "goff 18 riu 16 gl 16 upl 8 minl 16 maxl 16 inv 44 rof 8 sp 28 wl 12 ob 8 off 80 so 28 fo 16",
+    F32: "pf 8 ci 16 c16 16 c3 4 cf 44 r4 4 dum 27 kk 72 kr 12 km 384 ks 384 kq 16 pen0 8 cap 48 kx 256 rf 128 rb 512 val 336 iw 512 "
+         "s1 28 s2 27 s3 27 tw 32 wr 32 ff 80 ow 32 olt 32 ys 256 dh0 1024 dh1 1024 dh2 1024 ef 128 ei 64 hr 68 eh0 384 eh1 448 eh2 512",
+    BF: "kper 128 mask 128 sin 544 p32 512 p16 128 pp 256 pr 256 dif 256 ones 516 hot 516 sb 512 sbl 512 str 544 stl 512 tt 1345 "
+        "xi 1024 ut 512 vt 512 bt0 512 bt1 512 bt2 512 zf 1120 zt 512 xt 1024 pe 768 gm 256 rw 64 nb 64 pk 32 nm 800 iv 800",
+    X4: "qe 512 qw 512 qb 384 qu 128 qu2 128 qv 128 qr 384 qf 264 qz 256 qx 256 lq0 128 lq1 128 lq2 128",
+    U8: "sw 512 spl 896 su 128 su2 128 sv 128 sr 384 sf 264 sz 256 sx 256 ls0 512 ls1 512 ls2 512",
 }
 SCRATCH = {k: ("sbuf", [128, int(w)], d) for d, s in _S.items() for k, w in zip(s.split()[::2], s.split()[1::2])}
 SCRATCH.update({k: ("sbuf", [128, a, b], d) for k, a, b, d in [
     ("xp", 4, PL, F32), ("pen", 3, 9, F32), ("fn", 3, 9, F32), ("cpa", 3, 8, F32), ("pq", 3, 16, F32),
     ("mk", 5, 96, BF), ("sc", 5, 96, BF), ("gs", 3, 272, BF), ("pin", 3, 256, BF)]})
 SCRATCH["ps"] = ("psum", [128, 4096], F32)
-SEMAPHORES = ["cV", "cS", "cP", "cG"] + ["d%d" % i for i in range(28)] + ["l%d" % i for i in range(12)] + \
+SEMAPHORES = ["cV", "cS", "cP", "cG"] + ["d%d" % i for i in range(40)] + ["l%d" % i for i in range(12)] + \
     ["a%s%d" % (k, t) for k in "bkrs" for t in range(3)]
 
 
@@ -168,8 +170,8 @@ def rank_program(g, core, T, topo):
         view = T[name][:, r[0]:r[1], lo:hi:st] if isinstance(r, tuple) else T[name][:, r, lo:hi:st]
         return (view, [(name, cols)], len(cols), False)
 
-    def plane(b, lo, hi, st=1):
-        return R("xp", b, lo, hi, st)
+    def plane(b, lo, hi):
+        return R("xp", b, lo, hi)
 
     def bank(k, lo=0, hi=128, st=1):
         return A("ps", 512 * k + lo, 512 * k + hi, st)
@@ -199,7 +201,7 @@ def rank_program(g, core, T, topo):
         return 0.5 if all(SCRATCH[o[1][0][0]][2] in (BF, U16) for o in os) else 1
 
     def span(i, f):
-        return (0.06, "g", i[2]) if i[3] else (0.0, "c", max(64.0, i[2] * f))
+        return (0.06, "g", i[2]) if i[3] else (0.03, "c", max(64.0, i[2] * f))
 
     def run(eng, f, outs, ins, busy, after=()):
         regs = [r for o in ins if isinstance(o, tuple) for r in o[1]]
@@ -235,15 +237,15 @@ def rank_program(g, core, T, topo):
         run("V", lambda: g.vector.transpose(o[0], i[0]), [o], [i], span(i, half(o, i)))
 
     def quant(q, s, i):
-        run("V", lambda: g.vector.quantize_mx(q[0], s[0], i[0]), [q, s], [i], (0.015, "c", 0.27 * i[2]))
+        run("V", lambda: g.vector.quantize_mx(q[0], s[0], i[0]), [q, s], [i], (0.015, "c", 0.25 * i[2]))
 
     def act(o, i, func=act_.Copy, scale=None, bias=None):
         kw = {}
         if scale is not None:
-            kw["scale"] = scale
+            kw["scale"] = ap(scale)
         if bias is not None:
             kw["bias"] = ap(bias)
-        run("S", lambda: g.scalar.activation(o[0], i[0], func, **kw), [o], [i, bias], span(i, 1))
+        run("S", lambda: g.scalar.activation(o[0], i[0], func, **kw), [o], [i, bias, scale], span(i, 1))
 
     def fill(o, c):
         act(o, A("ones", 0, o[2]), scale=c)
@@ -265,20 +267,26 @@ def rank_program(g, core, T, topo):
 
     def iota(o, pat, base=0, ch=0, whole=False, after=()):
         kw = {} if whole else {"allow_small_or_imprecise_dtypes": True}
-        run("G", lambda: g.iota(o[0], pat, base, ch, **kw), [o], [], (0.13, "c", 2 * o[2]), after)
+        run("G", lambda: g.iota(o[0], pat, base, ch, **kw), [o], [], (0.13, "c", 1.8 * o[2]), after)
+
+    def const(o, c, after=()):
+        iota(o, [[0, o[2]]], c, after=after)
 
     def keep(o, pat, op, base, ch=0, after=()):
         i = A("ones", 0, o[2])
-        run("G", lambda: g.affine_select(o[0], i[0], pat, op, 0.0, base, ch), [o], [i], (0.17, "c", 2 * o[2]), after)
+        run("G", lambda: g.affine_select(o[0], i[0], pat, op, 0.0, base, ch), [o], [i], (0.17, "c", 1.8 * o[2]), after)
 
-    def dma(eng, out, in_, outs=(), ins=(), more=0.0, quiet=(), **kw):
+    def dma(eng, out, in_, outs=(), ins=(), more=0.0, quiet=(), after=(), **kw):
         s = "d%d" % nxt["d"]
         nxt["d"] += 1
         issue(eng, lambda sem: queue[eng].dma_start(out, in_, **kw).then_inc(T.sem[sem], 16), list(outs), list(ins),
-              (0.0, "D" if eng == "G" else "d", 1), ("l", more), s, 16, [("q", nxt["send"])] if eng == "G" else [], quiet)
+              (0.0, "D" if eng == "G" else "d", 1), ("l", more), s, 16, after, quiet)
 
     def load(eng, o, src, more=0.0, quiet=()):
         dma(eng, o[0], src, outs=o[1], more=more, quiet=quiet)
+
+    def copy(o, i):
+        dma("Y", o[0], i[0], o[1], i[1], 2.0)
 
     def raw(o):
         return (o[0].bitcast(dt.uint8), o[1])
@@ -286,6 +294,7 @@ def rank_program(g, core, T, topo):
     mate = [T.cores[rank ^ s] for s in STEP]
     low = [rank < (rank ^ s) for s in STEP]
     own = [0 if lo else 8 for lo in low]
+    kinds = sorted(set(low))
 
     def send(t, kind, pairs, more):
         rid, pid = topo.addr(mate[t])[:2]
@@ -321,22 +330,31 @@ def rank_program(g, core, T, topo):
     for t in range(3):
         lands(t, "b", [A("lq%d" % t, 16, 128), A("ls%d" % t, 64, 512)])
         lands(t, "k", [K(t, 8 - own[t], 16 - own[t])])
-        lands(t, "r", [A("lq%d" % t, 128, 144), A("ls%d" % t, 512, 576)])
+        lands(t, "r", [A("lq%d" % t, 0, 16), A("ls%d" % t, 0, 64)])
         if t:
             lands(t, "s", [A("kr", 4 * t, 4 * t + 1)])
 
     def send_bulk(t):
         send(t, "b", [(raw(A("lq%d" % t, 16, 128)), raw(A("qb", 128 * t + 16, 128 * t + 128))),
-                      (A("ls%d" % t, 64, 512), A("spl", 128 * t + 192, 128 * t + 640))], 0.7)
+                      (A("ls%d" % t, 64, 512), A("spl", 272 - 128 * t, 720 - 128 * t))], 0.7)
 
     def send_root(t):
-        c = 128 * t
-        send(t, "r", [(raw(A("lq%d" % t, 128, 144)), raw(A("qr", c, c + 16))), (A("ls%d" % t, 512, 576), A("sr", c, c + 64))], 0.2)
+        c = 128 * t if t else 112
+        send(t, "r", [(raw(A("lq%d" % t, 0, 16)), raw(A("qr", c, c + 16))), (A("ls%d" % t, 0, 64), A("sr", c - 48, c + 16))], 0.2)
 
-    m_, m8_, p31_, h16_, b15_, bm_ = [A("pf", j, j + 1) for j in range(6)]
+    def far(t):
+        return A("lq%d" % t), A("ls%d" % t, 48, 176)
+
+    m_, m8_, q_, h_, b15_, bm_ = [A("pf", j, j + 1) for j in range(6)]
 
     def qb(t):
-        return A("qb", 128 * t, 128 * t + 128), A("spl", 512 + 128 * t, 640 + 128 * t)
+        return A("qb", 128 * t, 128 * t + 128), A("spl", 256 - 128 * t, 384 - 128 * t)
+
+    def qe(b):
+        return A("qe", 128 * b, 128 * b + 128), A("spl", 384 + 128 * b, 512 + 128 * b)
+
+    def qw(b):
+        return A("qw", 128 * b, 128 * b + 128), A("sw", 128 * b, 128 * b + 128)
 
     def qr(t):
         return A("qr", 128 * t, 128 * t + 128), A("sr", 128 * t, 128 * t + 128)
@@ -345,142 +363,147 @@ def rank_program(g, core, T, topo):
         return A("sp", lo, hi, st)
 
     def inv(t, k):
-        return A("inv%d" % int(low[t]), 0, k)
+        c = 22 * kinds.index(low[t])
+        return A("inv", c, c + k)
 
     def ends(t, k):
-        return A("end%d" % int(low[t]), 0, k)
+        c = 22 * kinds.index(low[t]) + 16
+        return A("inv", c, c + k)
 
-    load("Y", A("lw", 16, 32), T.ri[:], 0.3)
+    load("Y", A("lw", 16, 32), T.ri[:], 0.2)
     urgent(50.0)
-    load("S", A("lw", 32, 33), T.ro[:], 0.3)
+    load("S", A("lw", 32, 33), T.ro[:], 0.2)
     load("S", A("lw", 0, 16), T.le[:], 0.3)
-    load("Y", A("xi"), T.x[:], 1.7)
+    load("Y", A("xi"), T.x[:], 1.1)
     urgent(40.0)
-    load("S", A("ut"), T.u[:], 2.5)
-    load("Y", raw(A("qw")), T.wc[:], 4.0)
+    load("Y", A("ut"), T.u[:], 1.6)
+    urgent(30.0)
+    load("Y", raw(A("qw")), T.wc[:], 2.6)
     urgent(20.0)
-    load("Y", A("sw"), T.ws[:], 4.5)
+    load("Y", A("sw"), T.ws[:], 2.9)
 
     ms(A("ones"), 1.0)
     urgent(30.0)
-    iota(A("pi"), [[0, 2], [8, 2]], 0, 1, True)
+    iota(A("pi", 0, 2), [[16, 2]], 0, 2, True)
+    iota(A("pi", 2, 3), [[0, 1]], 0, 1, True)
     iota(A("ci"), [[1, 16]])
+    iota(A("c16"), [[16, 16]])
     iota(A("kper"), [[0, 8], [1, 16]])
     keep(A("p16"), [[0, 8], [1, 16]], op_.is_ge, -1)
     keep(A("hot"), [[-1, 516]], op_.is_equal, 3, 4)
     ms(A("sin"), 0.0)
     fill(A("p32"), 1.0)
     fill(A("p32", 0, 512, 32), 0.0)
-    ms(A("zf", 64, 608), 0.0)
-    fill(A("zf", 608, 1120), 0.0)
-    ts(A("pj", 0, 2), A("pi", 0, 2), 15, op_.bitwise_and)
-    ts(A("pj", 2, 3), A("pi", 2, 3), 31, op_.bitwise_and)
-    ts(A("pj", 3, 4), A("pi", 2, 3), 16, op_.bitwise_and)
-    cp(A("pf", 0, 4), A("pj"))
-    cp(A("bl", 0, 32, 2), A("ci"))
-    cp(A("bl", 1, 32, 2), A("ci"))
-    fill(A("str", 512, 544), 256.0)
-    fill(A("tt", 256, 2 * TB, TB), 256.0)
-    fill(A("tt", 784, 785), 256.0)
+    fill(A("zf", 544, 1056), 0.0)
+    ts(A("pj", 0, 3), A("pi", 0, 3), 31, op_.bitwise_and)
+    ts(A("pf", 0, 3), A("pj", 0, 3), 0.5, op_.mult)
+    act(b15_, m_, act_.Identity, -1.0, 15.0)
+    act(h_, q_, act_.Identity, 2.0, b15_)
+    const(A("str", 512, 544), 256)
+    const(A("tt", 256, TB), 256)
+    const(A("tt", TB + 256, 2 * TB), 256)
+    const(A("tt", 2 * TB + 256, 1345, TB), 256)
     ms(A("sp"), 256)
     ts(A("mask"), A("kper"), m_, op_.is_equal)
-    ts(A("gl"), A("ci"), 32.0, op_.mult, p31_, op_.add)
-    ts(A("upl"), A("ci", 0, 8), 16.0, op_.mult)
-    fill(R("xp", (0, 4), 256, 288), 0.0)
+    ts(A("gl"), A("c16"), q_, op_.add, 2.0, op_.mult)
+    cp(A("upl"), A("c16", 0, 8))
     for b in range(4):
-        quant(A("qe", 128 * b, 128 * b + 128), A("spl", 128 * b, 128 * b + 128), A("hot", 3 - b, 515 - b))
-    act(b15_, m_, act_.Identity, -1.0, 15.0)
-    act(bm_, m_, act_.Identity, 2.0, 256.0)
+        quant(*qe(b), A("hot", 3 - b, 515 - b))
+    act(bm_, m_, act_.Identity, 4.0, -64.0)
     ts(A("minl"), A("ci"), b15_, op_.min)
     ts(A("maxl"), A("ci"), b15_, op_.max)
-    for lo in sorted(set(low)):
-        z_ = A("pf", 6 + lo, 7 + lo)
+    for j, lo in enumerate(kinds):
+        z_, c = A("pf", 6 + j, 7 + j), 22 * j
         act(z_, A("mask", 0, 1), scale=8.0 if lo else 16.0)
-        ts(A("inv%d" % lo), A("ones", 0, 16), z_, op_.mult, m8_ if lo else m_, op_.add)
-        if lo in low[:2]:
-            ts(A("end%d" % lo), A("inv%d" % lo), 16.0, op_.mult, 15.0, op_.add)
-    fill(A("pr"), 1.0)
-    fill(A("pr", 15, 241, 15), -1.0)
-    fill(A("pr", 0, 256, 16), 0.0)
+        act(A("cf", c, c + 16), A("ones", 0, 16), act_.Identity, z_, m8_ if lo else m_)
+        act(A("cf", c + 16, c + 22), A("cf", c, c + 6), act_.Identity, 16.0, 15.0)
+    cp(A("inv", 0, 22 * len(kinds)), A("cf", 0, 22 * len(kinds)))
+    for o in [A("zf", 0, 272), A("zf", 272, 544), A("zt", 0, 128), A("bt1", 0, 64), A("bt2", 0, 64), A("nb")]:
+        copy(o, A("zf", 544, 544 + o[2]))
+    for o in [A("pr"), R("pin", 0), R("pin", 1), R("pin", 2), A("rw")]:
+        copy(o, A("ones", 0, o[2]))
     fill(A("dif"), -16.0)
-    fill(A("dif", 0, 256, 16), 112.0)
-    fill(A("dif", 7, 256, 16), -32.0)
     act(A("dif", 15, 256, 16), A("ones", 0, 16), act_.Identity, 240.0, m_)
-    fill(R("gs", (0, 3), 256, 272), 1.0)
-    fill(A("rw"), 1.0)
-    fill(A("nb"), 0.0)
-    fill(R("sc", 1, 15, 16), 0.0)
-    fill(R("sc", 4, 63, 64), 256.0)
-    fill(A("bt1", 0, 64), 0.0)
-    fill(A("bt2", 0, 64), 0.0)
-    fill(A("zt", 0, 128), 0.0)
-    a, b = sorted(out_keys(t, 0, 1)[1][0][1] for t in (1, 2))
-    a, b = sorted([min(a), min(b)])
+    a, b = sorted(min(out_keys(t, 0, 1)[1][0][1]) for t in (1, 2))
     fill(A("kk", a, b + 1, b - a), -3e29)
-    for t in range(3):
-        fill(A("cap", 16 * t, 16 * t + 16), 10.0 if low[t] else 2.0)
 
     cp(A("sin", 0, 512, 32), A("lw", 16, 32))
     ts(A("gt1", 0, 17), A("lw", 16, 33), 496, op_.bitwise_and)
-    act(A("sbl"), ind(A("lw", 0, 16), A("bl")))
     ts(A("r4", 0, 1), A("lw", 32, 33), 4.0, op_.mult)
     scan(A("sb"), A("p32"), A("sin", 0, 512))
     tt(A("gt2", 0, 17), A("gt1", 0, 17), A("lw", 16, 33), op_.add)
     ts(A("rof", 0, 8, 2), A("ci", 0, 4), A("r4", 0, 1), op_.add)
     turn(A("str", 0, 512), A("sb"))
-    ts(A("goff", 0, 17), A("gt2", 0, 17), h16_, op_.add)
-    ts(sp(0, 19, 18), A("ones", 0, 2), A("r4", 0, 1), op_.mult, 0.25, op_.mult)
+    ts(A("goff", 0, 17), A("gt2", 0, 17), h_, op_.add, -15.0, op_.add)
+    ts(sp(0, 19, 9), A("ones", 0, 3), A("r4", 0, 1), op_.mult, 0.25, op_.mult)
     for b in range(4):
-        act(A("zf", b, 64, 4), ind(A("xi"), A("rof", 2 * b, 2 * b + 1)))
-    quant(*qr(0), A("zf", 0, 512))
+        act(A("zf", 1056 + b, 1120, 4), ind(A("xi"), A("rof", 2 * b, 2 * b + 1)))
+    quant(*qr(0), A("zf", 608, 1120))
     send_root(0)
+    urgent(UP0)
     behind = [("q", nxt["send"])]
-    act(A("tt", 0, 256), ind(A("str"), A("goff", 0, 16)))
+
+    def table(k, n=257):
+        return A("tt", TB * k, TB * k + n)
+
+    cp(A("riu"), A("lw", 16, 32))
+    act(table(1, 256), ind(A("str"), A("goff", 0, 16)))
+    act(table(2, 256), ind(table(1), A("riu")))
+    act(table(3, 256), ind(table(2), A("riu")))
+    cp(A("sin", 0, 512, 32), A("lw", 0, 16))
+    scan(A("sbl"), A("p32"), A("sin", 0, 512))
     turn(A("stl"), A("sbl"))
-    act(A("tt", 528, 784), ind(A("stl"), A("gl")))
-    act(A("tt", TB, TB + 256), ind(A("str"), A("gl")))
+    act(table(4, 256), ind(A("stl"), A("gl")))
+    act(table(0, 256), ind(A("str"), A("gl")))
     for b in range(4):
         act(plane(b, 0, 256), A("xi", b, 1024, 4), scale=0.5)
     quant(A("qu"), A("su"), A("ut"))
     words = ind(A("qu"), A("upl"), True)
     run("V", lambda: g.vector.tensor_copy(T.qu2[:].bitcast(dt.uint32), words[0]), [A("qu2")], [words], span(words, 1))
     act(A("su2"), ind(A("su"), A("upl")))
-    keep(A("pp"), [[0, 16], [1, 16]], op_.is_ge, -2)
-    iota(R("cpa", (0, 3)), [[0, 3], [1, 8]], -5)
+    const(R("xp", (0, 4), 256, 272), 0)
+    keep(A("pp"), [[0, 16], [1, 16]], op_.is_ge, -2, after=behind)
+    iota(R("cpa", (0, 3)), [[0, 3], [1, 8]], -5, after=behind)
+    iota(A("c3", 0, 3), [[TB, 3]])
+    const(A("pr", 15, 241, 15), -1, behind)
+    const(A("pr", 0, 256, 16), 0, behind)
+    const(R("gs", (0, 3), 256, 272), 1, behind)
+    const(R("sc", 4, 95, 96), 256)
+    const(A("hr", 64, 68), 0, behind)
     for t in range(3):
-        iota(R("pin", t), [[0, 256]], 1, after=behind)
+        const(A("cap", 16 * t, 16 * t + 16), 10 if low[t] else 2, behind)
         if low[t]:
-            fill(R("pin", t, 8, 256, 16), -15.0)
+            const(R("pin", t, 8, 256, 16), -15, behind)
+            if t and PATCH:
+                const(K(t, 0, 1), 0, behind)
 
-    def look(row, parts):
-        for j, win, off in parts:
-            tt(R("mk", row, 16 * j, 16 * (j + off[2])), ind(win, off), A("mask", 0, 16 * off[2]), op_.mult)
-        lo, hi = 16 * parts[0][0], 16 * (parts[-1][0] + parts[-1][2][2])
+    def look(row, j, win, off):
+        lo, hi = 16 * j, 16 * (j + off[2])
+        tt(R("mk", row, lo, hi), ind(win, off), A("mask", 0, hi - lo), op_.mult)
         scan(R("sc", row, lo, hi), A("p16", 0, hi - lo), R("mk", row, lo, hi))
 
-    def end(row, j0, j1, st=1):
-        return R("sc", row, 16 * j0 + 15, 16 * j1, 16 * st)
+    def end(row, j0, j1):
+        return R("sc", row, 16 * j0 + 15, 16 * j1, 16)
 
-    r2, r21, left = A("tt", 0, TB), A("tt", 0, 2 * TB), A("tt", 528, 785)
-    look(1, [(1, A("str"), A("goff", 16, 17))])
-    cp(sp(1, 2), end(1, 1, 2))
-    look(0, [(0, r2, sp(0, 2))])
-    cp(sp(2, 4), end(0, 0, 2))
-    look(1, [(2, left, sp(0, 2)), (4, r2, sp(2, 4))])
-    cp(A("wl", 2, 6), end(1, 2, 6))
-    ts(A("wl", 0, 2), end(1, 2, 4), float(TB), op_.add)
-    look(2, [(0, r21, A("wl", 0, 6))])
-    cp(sp(4, 8), end((1, 3), 4, 6))
-    cp(A("wl", 6, 10), end(2, 0, 4))
-    look(3, [(0, r2, A("wl", 6, 10))])
-    cp(A("wl", 10, 13), end(3, 0, 3))
-    look(4, [(0, r2, A("wl", 10, 13))])
-    cp(sp(9, 17), end((1, 5), 0, 3, 2))
-    cp(sp(19, 27), end((1, 5), 1, 4, 2))
+    look(0, 0, A("str"), A("goff", 16, 17))
+    ts(sp(1, 20, 18), A("ones", 0, 2), end(0, 0, 1), op_.mult)
+    look(0, 1, table(1), sp(0, 2))
+    cp(sp(2, 4), end(0, 1, 3))
+    look(1, 0, table(3), sp(0, 4))
+    cp(sp(4, 8), end(1, 0, 4))
+    look(2, 0, table(4), sp(0, 2))
+    for j in range(2):
+        ts(A("wl", 3 * j, 3 * j + 3), A("c3", 0, 3), end(2, j, j + 1), op_.add)
+    cp(sp(10, 21, 10), end(2, 0, 2))
+    look(3, 0, table(0, 2 * TB + 257), A("wl", 0, 6))
+    cp(A("wl", 6, 11), end(3, 0, 5))
+    look(4, 0, table(2), A("wl", 6, 11))
+    cp(sp(11, 17), end((3, 5), 0, 3))
+    cp(sp(21, 27), end((3, 5), 3, 6))
 
-    def spine_tile(t, off, i0, hi, engines):
+    def spine_tile(t, off, i0, engines):
         for b in range(4):
-            mul(engines[b], A("bt%d" % t, 64 * i0 + b, 64 * (i0 + off[2]), 4), ind(plane(b, 0, hi), off), 2.0)
+            mul(engines[b], A("bt%d" % t, 64 * i0 + b, 64 * (i0 + off[2]), 4), ind(plane(b, 0, 272), off), 2.0)
 
     def keys(t, pen):
         i0, c = int(t > 0), 128 * t
@@ -498,18 +521,28 @@ def rank_program(g, core, T, topo):
 
     def unpack(t, q, s, to):
         for b in range(4):
-            mm(b, (A("qe", 128 * b, 128 * b + 128), A("spl", 128 * b, 128 * b + 128), q, s))
+            mm(b, (*qe(b), q, s))
         for b in range(4):
             act(A("dh%d" % t, 256 * b + to, 256 * b + to + 128), bank(b), scale=0.5)
 
-    def far(t):
-        return A("lq%d" % t, 16, 144), A("ls%d" % t, 400, 528)
-
-    def order(t):
+    def pairs(t):
         for j in range(2):
             act(A("kx", 128 * j, 128 * j + 128), ind(K(t, 0, 16), A("maxl", 8 * j, 8 * j + 8)))
         for j in range(2):
             tt(A("gm", 128 * j, 128 * j + 128), ind(K(t, 0, 16), A("minl", 8 * j, 8 * j + 8)), A("kx", 128 * j, 128 * j + 128), op_.is_ge)
+
+    def order(t):
+        s = K(t, own[t], own[t] + 1)
+        if not PATCH or not t:
+            pairs(t)
+        elif low[t]:
+            ts(A("gm", 15, 256, 16), K(t, 0, 16), s, op_.is_le)
+            ts(A("gm", 0, 15), K(t, 1, 16), s, op_.is_le)
+        else:
+            ts(A("gm", 7, 128, 16), K(t, 0, 8), s, op_.is_ge)
+            ts(A("gm", 135, 256, 16), K(t, 8, 16), s, op_.is_le)
+            ts(A("gm", 128, 135), K(t, 9, 16), s, op_.is_le)
+            ts(A("gm", 136, 144), K(t, 0, 8), s, op_.is_ge)
         scan(R("gs", t, 0, 256), A("pr"), A("gm"))
 
     def insert(t):
@@ -550,7 +583,7 @@ def rank_program(g, core, T, topo):
             tt(A(tile, 64 * i0 + b, 64 * i0 + 4 * n, 4), ind(window(t, b), ln), A(buf, c + n * b, c + n * b + n), op_.add)
         quant(q, s, A(tile, 0, 512))
         for b in range(4):
-            mm(k0 + b, (A("qw", 128 * b, 128 * b + 128), A("sw", 128 * b, 128 * b + 128), q, s))
+            mm(k0 + b, (*qw(b), q, s))
 
     def relu(eng, o, i, c):
         if eng == "S":
@@ -564,13 +597,12 @@ def rank_program(g, core, T, topo):
         for b in range(4):
             act(A("ef", b, 4 * n, 4), ind(window(t, b), la))
         for b in range(4):
-            tt(A("zf", 88 + b, 64 + 32 * n, 32), ind(window(t, b), ln), A("ef", b, 4 * n, 4), op_.add)
+            tt(A("zf", 24 + b, 32 * n, 32), ind(window(t, b), ln), A("ef", b, 4 * n, 4), op_.add)
         act(A("ei"), A("ef", 0, 64), scale=2.0)
-        quant(A("qf", 0, w), A("sf", 0, w), A("zf", 64, 64 + 4 * w))
+        quant(A("qf", 0, w), A("sf", 0, w), A("zf", 0, 4 * w))
         for i in range(la[2]):
             c = [128 * i + 6 - 2 * b for b in range(4)]
-            mm(4 + i, *[(A("qw", 128 * b, 128 * b + 128), A("sw", 128 * b, 128 * b + 128), A("qf", c[b], c[b] + 128), A("sf", c[b], c[b] + 128))
-                        for b in range(4)])
+            mm(4 + i, *[(*qw(b), A("qf", c[b], c[b] + 128), A("sf", c[b], c[b] + 128)) for b in range(4)])
         relu(RELU, A("rf", 0, 64), bank(4, 0, 128, 2), 0.03125)
         tt(A("bt%d" % (t + 1), 0, 64), A("rf", 0, 64), A("ei"), op_.add)
         quant(*qr(t + 1), A("bt%d" % (t + 1)))
@@ -581,14 +613,17 @@ def rank_program(g, core, T, topo):
         red(mine, A("kq"))
         send(t + 1, "s", [(A("kr", 4 * t + 4, 4 * t + 5), mine)], 0.0)
 
-    def long_road(t, la, ln, k0):
-        i0, hi = FAST[t], [384, 496][t]
+    def long_road(t, la, ln, k0, after):
+        i0, hi = FAST[t], [368, 480][t]
         n = 16 * (8 - i0)
         layer(t, i0, la, ln, "eh%d" % t, 0, "zt", 1, k0)
+        o = R("xp", (0, 4), hi - n, hi)
         for b in range(4):
             relu("S", plane(b, hi - n, hi), bank(k0 + b, 128 - n, 128), 0.015625)
-        o = R("xp", (0, 4), hi - n, hi)
-        dma("G", o[0], T["eh%d" % t][:], o[1], A("eh%d" % t)[1], 1.5, accum_op=op_.add)
+            if ADD[t] == "V":
+                tt(plane(b, hi - n, hi), plane(b, hi - n, hi), A("eh%d" % t, n * b, n * b + n), op_.add)
+        if ADD[t] == "G":
+            dma("G", o[0], T["eh%d" % t][:], o[1], A("eh%d" % t)[1], 1.5, after=after, accum_op=op_.add)
 
     def scatter(lo, hi, v0):
         o = ind(A("iw"), A("so", lo, hi))
@@ -598,16 +633,16 @@ def rank_program(g, core, T, topo):
     def off(lo, hi, st=1):
         return A("off", lo, hi, st)
 
-    spine_tile(0, sp(0, 8), 0, 272, B0)
+    spine_tile(0, sp(0, 8), 0, B0)
     ts(A("pen0"), sp(0, 8), 256.0, op_.is_equal, BIG, op_.mult)
     keys(0, A("pen0"))
     behind = [("q", nxt["send"])]
-    iota(A("val", 0, 16), [[1, 16]], 496, after=behind)
-    iota(A("val", 16, 32), [[-1, 16]], -512, after=behind)
-    iota(A("val", 32, 240), [[1, 208]], 288, after=behind)
-    iota(A("val", 240, 336), [[1, 96]], 528, after=behind)
+    iota(A("val", 0, 16), [[1, 16]], 480, after=behind)
+    iota(A("val", 16, 32), [[-1, 16]], -496, after=behind)
+    iota(A("val", 32, 240), [[1, 208]], 272, after=behind)
+    iota(A("val", 240, 336), [[1, 96]], 512, after=behind)
     iota(A("iw", 0, 256), [[1, 256]], after=behind)
-    iota(A("iw", 256, 512), [[0, 256]], after=behind)
+    copy(A("iw", 256, 512), A("iw", 0, 256))
     iota(A("s3"), [[0, 3], [16, 9]], 256, after=behind)
     act(A("dum"), A("s3"), act_.Identity, 1.0, m_)
     unpack(0, *qb(0), 128)
@@ -619,26 +654,31 @@ def rank_program(g, core, T, topo):
     tt(R("pin", (0, 3), 1, 256, 16), R("pq", (0, 3)), A("cap"), op_.min)
     for t in range(3):
         scan(A("pe", 256 * t, 256 * t + 256), A("pp"), R("pin", t))
-    spine_tile(1, sp(10, 17), 1, 272, "SSSS")
+    spine_tile(1, sp(10, 17), 1, "SSSS")
     keys(1, R("pen", 1, 1, 8))
-    ts(A("ob", 0, 1), sp(1, 2), 256.0, op_.not_equal, bm_, op_.add)
-    spine_tile(2, sp(20, 26), 2, 272, "SSSS")
+    ts(A("r4", 1, 2), sp(1, 2), 256.0, op_.not_equal, bm_, op_.mult)
+    ts(A("ob", 0, 8, 2), A("ci", 0, 4), A("r4", 1, 2), op_.add, 64.0, op_.add)
+    spine_tile(2, sp(20, 26), 2, "SSSS")
     order(0)
+    if PATCH:
+        pairs(1)
     unpack(0, *far(0), 0)
     invert(ind(R("gs", 0), ends(0, 2)), wanted(0, 0, 2), off(0, 4))
     short_road(0, off(0, 2), off(2, 4))
 
     load("Y", A("vt"), T.v[:], 0.7, A("kq")[1])
+    order(1)
     unpack(1, *qr(1), 128)
     relu("S", A("rf", 64, 128), bank(5, 0, 128, 2), 0.015625)
-    tt(A("hr"), A("rf", 64, 128), A("ef", 64, 128), op_.add)
+    tt(A("hr", 0, 64), A("rf", 64, 128), A("ef", 64, 128), op_.add)
     for b in range(4):
-        act(plane(b, 257, 288, 2), A("hr", b, 64, 4))
-    spine_tile(2, A("ob", 0, 1), 1, 288, "SSSS")
+        act(A("bt2", 64 + b, 128, 4), ind(A("hr"), A("ob", 2 * b, 2 * b + 1)), scale=2.0)
     keys(2, R("pen", 2, 1, 8))
-    order(1)
+    behind = [("q", nxt["send"])]
     for j, want in enumerate(wanted(1, 0, 1)):
         tt(A("pk", 16 * j, 16 * j + 16), ind(R("gs", 1), ends(1, 1)), want, op_.subtract)
+    if PATCH:
+        pairs(2)
     unpack(1, *far(1), 0)
     insert(1)
     invert(ind(A("nb", 0, 32), inv(1, 2)), [A("pk")], off(4, 8, 2))
@@ -657,7 +697,7 @@ def rank_program(g, core, T, topo):
     urgent(6.0)
     act(f1, A("wr", 0, 16), act_.Abs)
     cp(A("fo"), f1)
-    ts(f3, A("wr", 0, 16), 288.0, op_.is_ge)
+    ts(f3, A("wr", 0, 16), 272.0, op_.is_ge)
     tt(f4, A("lw", 16, 32), A("lw", 0, 16), op_.subtract)
     tt(f5, f3, f4, op_.mult)
     tt(A("ow", 0, 16), A("lw", 0, 16), f5, op_.add)
@@ -666,12 +706,12 @@ def rank_program(g, core, T, topo):
     for h in range(2):
         dma("Y", T.ol[h::2, :], T.olt[:, 16 * h:16 * h + 16], ins=A("olt")[1], more=1.0)
 
-    invert(ind(R("gs", 0), ends(0, 6)), wanted(0, 2, 8), off(8, 20))
-    long_road(0, off(8, 14), off(14, 20), 0)
-    unpack(2, *qr(2), 128)
     order(2)
+    invert(ind(R("gs", 0), ends(0, 6)), wanted(0, 2, 8), off(8, 20))
+    long_road(0, off(8, 14), off(14, 20), 0, behind)
+    unpack(2, *qr(2), 128)
     invert(ind(ranks(1), inv(1, 16)), [A("pe", 256, 512)], off(21, 37))
-    long_road(1, off(22, 29), off(30, 37), 4)
+    long_road(1, off(22, 29), off(30, 37), 4, [("q", nxt["send"])])
     quant(A("qv"), A("sv"), A("vt"))
     unpack(2, *far(2), 0)
     insert(2)
@@ -683,7 +723,7 @@ def rank_program(g, core, T, topo):
         for b in range(4):
             c = 256 * h + 64 * b
             relu("S", A("rb", c, c + 64), bank(k0 + b, 64 * h, 64 * h + 64), 0.015625)
-            tt(plane(b, 496 + 64 * h, 560 + 64 * h), A("rb", c, c + 64), A("eh2", c, c + 64), op_.add)
+            tt(plane(b, 480 + 64 * h, 544 + 64 * h), A("rb", c, c + 64), A("eh2", c, c + 64), op_.add)
     for h in range(2):
         c = 128 * h
         for b in range(4):

from concourse.bass import DstId, RemoteDMATransfer
from concourse.mybir import dt, AluOpType, AxisListType, ActivationFunctionType

BF, F32, I32, U16, X4, U8 = "bfloat16", "float32", "int32", "uint16", "float8_e4m3fn_x4", "uint8"
PL = 608
TB = 272
BIG = 2.0 ** 90
STEP = [1, 2, 4]
FAST = [2, 1]
LAST = ["SSSV", "SSVV"]
B0 = "VSVS"
RELU = "S"
PATCH = False
ADD = "GV"
UP0 = 1.5
PACE = {"c": 0.00105, "g": 0.0015, "s": 0.0035, "p": 0.0006, "wake": 0.14, "l": 1.3, "r": 1.4, "i": 0.4, "first": 2.0, "d": 0.1, "D": 1.0}
AHEAD = 0.4
TRIES = 2000
PACES = [{}, {"c": 0.0009, "g": 0.001, "s": 0.0016, "p": 0.00045, "wake": 0.08, "l": 1.0, "r": 1.0, "i": 0.3, "first": 1.5},
         {"c": 0.0014, "g": 0.0024, "s": 0.0065, "p": 0.0009}, {"r": 2.6, "i": 0.8, "first": 3.0, "l": 2.0, "D": 1.5},
         {"wake": 0.2, "d": 0.2}]

_S = {
    I32: "lw 36 pi 4 pj 4 gt1 20 gt2 20",
    U16: "goff 18 riu 16 gl 16 upl 8 minl 16 maxl 16 inv 44 rof 8 sp 28 wl 12 ob 8 off 80 so 28 fo 16",
    F32: "pf 8 ci 16 c16 16 c3 4 cf 44 r4 4 dum 27 kk 72 kr 12 km 384 ks 384 kq 16 pen0 8 cap 48 kx 256 rf 128 rb 512 val 336 iw 512 "
         "s1 28 s2 27 s3 27 tw 32 wr 32 ff 80 ow 32 olt 32 ys 256 dh0 1024 dh1 1024 dh2 1024 ef 128 ei 64 hr 68 eh0 384 eh1 448 eh2 512",
    BF: "kper 128 mask 128 sin 544 p32 512 p16 128 pp 256 pr 256 dif 256 ones 516 hot 516 sb 512 sbl 512 str 544 stl 512 tt 1345 "
        "xi 1024 ut 512 vt 512 bt0 512 bt1 512 bt2 512 zf 1120 zt 512 xt 1024 pe 768 gm 256 rw 64 nb 64 pk 32 nm 800 iv 800",
    X4: "qe 512 qw 512 qb 384 qu 128 qu2 128 qv 128 qr 384 qf 264 qz 256 qx 256 lq0 128 lq1 128 lq2 128",
    U8: "sw 512 spl 896 su 128 su2 128 sv 128 sr 384 sf 264 sz 256 sx 256 ls0 512 ls1 512 ls2 512",
}
SCRATCH = {k: ("sbuf", [128, int(w)], d) for d, s in _S.items() for k, w in zip(s.split()[::2], s.split()[1::2])}
SCRATCH.update({k: ("sbuf", [128, a, b], d) for k, a, b, d in [
    ("xp", 4, PL, F32), ("pen", 3, 9, F32), ("fn", 3, 9, F32), ("cpa", 3, 8, F32), ("pq", 3, 16, F32),
    ("mk", 5, 96, BF), ("sc", 5, 96, BF), ("gs", 3, 272, BF), ("pin", 3, 256, BF)]})
SCRATCH["ps"] = ("psum", [128, 4096], F32)
SEMAPHORES = ["cV", "cS", "cP", "cG"] + ["d%d" % i for i in range(40)] + ["l%d" % i for i in range(12)] + \
    ["a%s%d" % (k, t) for k in "bkrs" for t in range(3)]


def timed(ops, sent, pace):
    busy = [o["busy"][0] + o["busy"][2] * pace[o["busy"][1]] for o in ops]
    lag = [pace[o["lag"][0]] + o["lag"][1] if o["lag"] else 0.0 for o in ops]
    edges = [[] for _ in ops]
    for k, o in enumerate(ops):
        for d in o["deps"]:
            if isinstance(d, tuple):
                edges[k].append((sent[d[1]], lag[sent[d[1]]]) if d[0] == "a" else (d[1], 0.0))
            else:
                edges[k].append((d, lag[d] + pace["wake"]))
        edges[k].sort()
    return busy, lag, edges


def arrange(ops, sent):
    n = len(ops)
    busy, lag, edges = timed(ops, sent, PACE)
    later = [[] for _ in ops]
    for k in range(n):
        for d, w in edges[k]:
            later[d].append((k, w))
    chain, left = [None] * n, [len(e) for e in later]
    todo = [k for k in range(n) if not left[k]]
    while todo:
        k = todo.pop()
        chain[k] = ops[k]["up"] + busy[k] + max([lag[k]] + [w + chain[j] for j, w in later[k]])
        for d, w in edges[k]:
            left[d] -= 1
            if not left[d]:
                todo.append(d)
    free, done, plan = {q: 0.0 for q in "VSPGY"}, {}, []
    ready = {q: {} for q in free}
    left = [len(e) for e in edges]
    for k in range(n):
        if not left[k]:
            ready[ops[k]["eng"]][k] = 0.0
    while len(plan) < n:
        now, eng = min((max(free[q], min(r.values())), q) for q, r in ready.items() if r)
        mine = ready[eng]
        k = min((k for k in mine if mine[k] <= now), key=lambda k: (-chain[k], k))
        soon = [j for j in mine if chain[j] > chain[k] + busy[k] and mine[j] < now + AHEAD * busy[k]]
        if soon:
            k = min(soon, key=lambda j: (mine[j], j))
        done[k] = free[eng] = max(now, mine.pop(k)) + busy[k]
        plan.append(k)
        for j, w in later[k]:
            left[j] -= 1
            if not left[j]:
                ready[ops[j]["eng"]][j] = max(done[d] + x for d, x in edges[j])
    return plan


def clock(eng, times, plan):
    busy, lag, edges = times
    free, last, done, why, end, k0 = dict.fromkeys("VSPGY", 0.0), {}, {}, {}, 0.0, None
    for k in plan:
        e = eng[k]
        s, w, q = free[e], last.get(e), True
        for d, x in edges[k]:
            if done[d] + x > s:
                s, w, q = done[d] + x, d, False
        done[k] = free[e] = s + busy[k]
        last[e], why[k] = k, (w, q)
        if done[k] + lag[k] > end:
            end, k0 = done[k] + lag[k], k
    pairs = []
    while k0 is not None:
        w, q = why[k0]
        if q and w is not None:
            pairs.append((w, k0))
        k0 = w
    return end, pairs


def polish(ops, sent, plan):
    eng = [o["eng"] for o in ops]
    times = [timed(ops, sent, {**PACE, **p}) for p in PACES]
    pre = [set(d for d, x in e) for e in times[0][2]]
    now = [clock(eng, t, plan) for t in times]
    base = [x[0] for x in now]
    best, s = float(len(now)), 1
    for it in range(TRIES):
        r = []
        for _ in range(3):
            s = (s * 1103515245 + 12345) % 2147483648
            r.append(s >> 8)
        pairs = now[r[0] % len(now)][1]
        j, k = pairs[r[1] % len(pairs)]
        a, b = plan.index(j), plan.index(k)
        moved, keep, late = {j}, [], [j]
        for x in plan[a + 1:b]:
            if pre[x] & moved:
                moved.add(x)
                late.append(x)
            else:
                keep.append(x)
        if pre[k] & moved:
            continue
        tail, more, t = plan[b + 1:], r[2] % 6, 0
        while more and t < len(tail) and not pre[tail[t]] & moved:
            more -= eng[tail[t]] == eng[k]
            t += 1
        new = plan[:a] + keep + [k] + tail[:t] + late + tail[t:]
        then = [clock(eng, x, new) for x in times]
        c = sum(x[0] / y for x, y in zip(then, base))
        if c <= best + 0.0015 * max(0.0, 1 - 1.3 * it / TRIES):
            plan, now, best = new, then, c
    return plan


def rank_program(g, core, T, topo):
    rank = T.rank_of(core)
    if rank is None:
        return
    op_, act_ = AluOpType, ActivationFunctionType
    queue = {"V": g.vector, "S": g.scalar, "P": g.tensor, "G": g, "Y": g.sync}
    ops, past, nxt, arrive, sent = [], {}, {"d": 0, "l": 0, "send": None}, {}, {}

    def A(name, lo=0, hi=None, st=1):
        hi = SCRATCH[name][1][1] if hi is None else hi
        cols = frozenset([lo // 512]) if name == "ps" else frozenset(range(lo, hi, st))
        return (T[name][:, lo:hi:st], [(name, cols)], len(range(lo, hi, st)), False)

    def R(name, r, lo=0, hi=None, st=1):
        w = SCRATCH[name][1][2]
        hi = w if hi is None else hi
        rows = range(*r) if isinstance(r, tuple) else [r]
        cols = frozenset(w * i + c for i in rows for c in range(lo, hi, st))
        view = T[name][:, r[0]:r[1], lo:hi:st] if isinstance(r, tuple) else T[name][:, r, lo:hi:st]
        return (view, [(name, cols)], len(cols), False)

    def plane(b, lo, hi):
        return R("xp", b, lo, hi)

    def bank(k, lo=0, hi=128, st=1):
        return A("ps", 512 * k + lo, 512 * k + hi, st)

    def ind(win, off, words=False):
        w = win[0].bitcast(dt.uint32) if words else win[0]
        return (w.indirect(off[0]), win[1] + off[1], 16 * off[2], True)

    def issue(eng, call, outs, ins, busy, lag=None, sem=None, n=1, after=(), quiet=(), up=0.0):
        deps = set(after)
        for regs, write in ((outs, True), (ins, False), (quiet, False)):
            for name, cols in regs:
                for c, w, who, e in past.get(name, []):
                    if (write or w or (name == "ps" and e != eng)) and not cols.isdisjoint(c):
                        deps.add(who)
        k = len(ops)
        ops.append({"eng": eng, "call": call, "deps": deps, "busy": busy, "lag": lag, "sem": sem, "n": n, "up": up})
        for regs, write in ((outs, True), (ins, False)):
            for name, cols in regs:
                past.setdefault(name, []).append((cols, write, k, eng))
        return k

    def urgent(x):
        ops[-1]["up"] = x

    def half(*os):
        return 0.5 if all(SCRATCH[o[1][0][0]][2] in (BF, U16) for o in os) else 1

    def span(i, f):
        return (0.06, "g", i[2]) if i[3] else (0.03, "c", max(64.0, i[2] * f))

    def run(eng, f, outs, ins, busy, after=()):
        regs = [r for o in ins if isinstance(o, tuple) for r in o[1]]
        issue(eng, lambda s: f().then_inc(T.sem[s], 1), [r for o in outs for r in o[1]], regs, busy, after=after)

    def ap(o):
        return o[0] if isinstance(o, tuple) else o

    def cp(o, i):
        run("V", lambda: g.vector.tensor_copy(o[0], i[0]), [o], [i], span(i, half(o, i)))

    def ms(o, c):
        run("V", lambda: g.vector.memset(o[0], c), [o], [], span(o, half(o)))

    def ts(o, i, s1, op0, s2=None, op1=None):
        w = span(i, half(o, i))
        if op1 is None:
            run("V", lambda: g.vector.tensor_scalar(o[0], i[0], ap(s1), None, op0), [o], [i, s1], w)
        else:
            run("V", lambda: g.vector.tensor_scalar(o[0], i[0], ap(s1), ap(s2), op0, op1), [o], [i, s1, s2], w)

    def tt(o, a, b, op):
        run("V", lambda: g.vector.tensor_tensor(o[0], a[0], b[0], op), [o], [a, b], span(a, 1 if a[1][0][0] == "ps" else 2))

    def scan(o, keep, add):
        run("V", lambda: g.vector.tensor_tensor_scan(o[0], keep[0], add[0], 0.0, op_.mult, op_.add), [o], [keep, add],
            span(add, half(o, keep, add)))

    def red(o, i):
        run("V", lambda: g.vector.tensor_reduce(o[0], i[0], AxisListType.X, op_.add), [o], [i], span(i, 1))

    def turn(o, i):
        run("V", lambda: g.vector.transpose(o[0], i[0]), [o], [i], span(i, half(o, i)))

    def quant(q, s, i):
        run("V", lambda: g.vector.quantize_mx(q[0], s[0], i[0]), [q, s], [i], (0.015, "c", 0.25 * i[2]))

    def act(o, i, func=act_.Copy, scale=None, bias=None):
        kw = {}
        if scale is not None:
            kw["scale"] = ap(scale)
        if bias is not None:
            kw["bias"] = ap(bias)
        run("S", lambda: g.scalar.activation(o[0], i[0], func, **kw), [o], [i, bias, scale], span(i, 1))

    def fill(o, c):
        act(o, A("ones", 0, o[2]), scale=c)

    def mul(eng, o, i, c):
        if eng == "S":
            act(o, i, act_.Copy, scale=c)
        else:
            ts(o, i, c, op_.mult)

    def mm(k, *sides):
        o = bank(k)

        def call():
            for j, (lq, ls, rq, rs) in enumerate(sides):
                last = g.tensor.matmul_mx(o[0], lq[0], ls[0], rq[0], rs[0], j == 0, j == len(sides) - 1)
            return last
        run("P", call, [o], [x for s in sides for x in s], (0.0, "p", 144 * len(sides)))

    def iota(o, pat, base=0, ch=0, whole=False, after=()):
        kw = {} if whole else {"allow_small_or_imprecise_dtypes": True}
        run("G", lambda: g.iota(o[0], pat, base, ch, **kw), [o], [], (0.13, "c", 1.8 * o[2]), after)

    def const(o, c, after=()):
        iota(o, [[0, o[2]]], c, after=after)

    def keep(o, pat, op, base, ch=0, after=()):
        i = A("ones", 0, o[2])
        run("G", lambda: g.affine_select(o[0], i[0], pat, op, 0.0, base, ch), [o], [i], (0.17, "c", 1.8 * o[2]), after)

    def dma(eng, out, in_, outs=(), ins=(), more=0.0, quiet=(), after=(), **kw):
        s = "d%d" % nxt["d"]
        nxt["d"] += 1
        issue(eng, lambda sem: queue[eng].dma_start(out, in_, **kw).then_inc(T.sem[sem], 16), list(outs), list(ins),
              (0.0, "D" if eng == "G" else "d", 1), ("l", more), s, 16, after, quiet)

    def load(eng, o, src, more=0.0, quiet=()):
        dma(eng, o[0], src, outs=o[1], more=more, quiet=quiet)

    def copy(o, i):
        dma("Y", o[0], i[0], o[1], i[1], 2.0)

    def raw(o):
        return (o[0].bitcast(dt.uint8), o[1])

    mate = [T.cores[rank ^ s] for s in STEP]
    low = [rank < (rank ^ s) for s in STEP]
    own = [0 if lo else 8 for lo in low]
    kinds = sorted(set(low))

    def send(t, kind, pairs, more):
        rid, pid = topo.addr(mate[t])[:2]
        eng = topo.engines(core, mate[t])
        k = len(eng) // len(pairs)
        far = T.sem["a%s%d" % (kind, t)]
        s = "l%d" % nxt["l"]
        nxt["l"] += 1
        if len(pairs) == 1:
            call = lambda sem: g.remote_dma(pairs[0][0][0], pairs[0][1][0], far, T.sem[sem], pid, rid, topo.mask(core, mate[t]))
        else:
            tr = [RemoteDMATransfer(dst_ids=[DstId(rid=rid, pnc=pid)], dma_engine_mask=sum(1 << e for e in eng[k * j:k * j + k]),
                                    remote_sem=far, src=b[0], dst=a[0]) for j, (a, b) in enumerate(pairs)]
            call = lambda sem: g.remote_dma_fused(tr, local_sem=T.sem[sem])
        before = [] if nxt["send"] is None else [("q", nxt["send"])]
        nxt["send"] = issue("G", call, [], [r for a, b in pairs for r in b[1]], (0.0, "i" if before else "first", 1), ("r", more),
                            s, len(eng), before, up=3.0 if kind in "rs" and t else 0.0)
        sent["a%s%d" % (kind, t)] = nxt["send"]

    def K(t, lo, hi):
        return A("kk", 16 * t + lo, 16 * t + hi)

    def out_keys(t, lo, hi):
        return A("kk", 48 + 8 * t + lo, 48 + 8 * t + hi) if low[t] else K(t, 8 + lo, 8 + hi)

    def lands(t, kind, places):
        s = "a%s%d" % (kind, t)
        arrive[s] = len(topo.engines(mate[t], core))
        for o in places:
            for name, cols in o[1]:
                past.setdefault(name, []).append((cols, True, ("a", s), "far"))

    for t in range(3):
        lands(t, "b", [A("lq%d" % t, 16, 128), A("ls%d" % t, 64, 512)])
        lands(t, "k", [K(t, 8 - own[t], 16 - own[t])])
        lands(t, "r", [A("lq%d" % t, 0, 16), A("ls%d" % t, 0, 64)])
        if t:
            lands(t, "s", [A("kr", 4 * t, 4 * t + 1)])

    def send_bulk(t):
        send(t, "b", [(raw(A("lq%d" % t, 16, 128)), raw(A("qb", 128 * t + 16, 128 * t + 128))),
                      (A("ls%d" % t, 64, 512), A("spl", 272 - 128 * t, 720 - 128 * t))], 0.7)

    def send_root(t):
        c = 128 * t if t else 112
        send(t, "r", [(raw(A("lq%d" % t, 0, 16)), raw(A("qr", c, c + 16))), (A("ls%d" % t, 0, 64), A("sr", c - 48, c + 16))], 0.2)

    def far(t):
        return A("lq%d" % t), A("ls%d" % t, 48, 176)

    m_, m8_, q_, h_, b15_, bm_ = [A("pf", j, j + 1) for j in range(6)]

    def qb(t):
        return A("qb", 128 * t, 128 * t + 128), A("spl", 256 - 128 * t, 384 - 128 * t)

    def qe(b):
        return A("qe", 128 * b, 128 * b + 128), A("spl", 384 + 128 * b, 512 + 128 * b)

    def qw(b):
        return A("qw", 128 * b, 128 * b + 128), A("sw", 128 * b, 128 * b + 128)

    def qr(t):
        return A("qr", 128 * t, 128 * t + 128), A("sr", 128 * t, 128 * t + 128)

    def sp(lo, hi, st=1):
        return A("sp", lo, hi, st)

    def inv(t, k):
        c = 22 * kinds.index(low[t])
        return A("inv", c, c + k)

    def ends(t, k):
        c = 22 * kinds.index(low[t]) + 16
        return A("inv", c, c + k)

    load("Y", A("lw", 16, 32), T.ri[:], 0.2)
    urgent(50.0)
    load("S", A("lw", 32, 33), T.ro[:], 0.2)
    load("S", A("lw", 0, 16), T.le[:], 0.3)
    load("Y", A("xi"), T.x[:], 1.1)
    urgent(40.0)
    load("Y", A("ut"), T.u[:], 1.6)
    urgent(30.0)
    load("Y", raw(A("qw")), T.wc[:], 2.6)
    urgent(20.0)
    load("Y", A("sw"), T.ws[:], 2.9)

    ms(A("ones"), 1.0)
    urgent(30.0)
    iota(A("pi", 0, 2), [[16, 2]], 0, 2, True)
    iota(A("pi", 2, 3), [[0, 1]], 0, 1, True)
    iota(A("ci"), [[1, 16]])
    iota(A("c16"), [[16, 16]])
    iota(A("kper"), [[0, 8], [1, 16]])
    keep(A("p16"), [[0, 8], [1, 16]], op_.is_ge, -1)
    keep(A("hot"), [[-1, 516]], op_.is_equal, 3, 4)
    ms(A("sin"), 0.0)
    fill(A("p32"), 1.0)
    fill(A("p32", 0, 512, 32), 0.0)
    fill(A("zf", 544, 1056), 0.0)
    ts(A("pj", 0, 3), A("pi", 0, 3), 31, op_.bitwise_and)
    ts(A("pf", 0, 3), A("pj", 0, 3), 0.5, op_.mult)
    act(b15_, m_, act_.Identity, -1.0, 15.0)
    act(h_, q_, act_.Identity, 2.0, b15_)
    const(A("str", 512, 544), 256)
    const(A("tt", 256, TB), 256)
    const(A("tt", TB + 256, 2 * TB), 256)
    const(A("tt", 2 * TB + 256, 1345, TB), 256)
    ms(A("sp"), 256)
    ts(A("mask"), A("kper"), m_, op_.is_equal)
    ts(A("gl"), A("c16"), q_, op_.add, 2.0, op_.mult)
    cp(A("upl"), A("c16", 0, 8))
    for b in range(4):
        quant(*qe(b), A("hot", 3 - b, 515 - b))
    act(bm_, m_, act_.Identity, 4.0, -64.0)
    ts(A("minl"), A("ci"), b15_, op_.min)
    ts(A("maxl"), A("ci"), b15_, op_.max)
    for j, lo in enumerate(kinds):
        z_, c = A("pf", 6 + j, 7 + j), 22 * j
        act(z_, A("mask", 0, 1), scale=8.0 if lo else 16.0)
        act(A("cf", c, c + 16), A("ones", 0, 16), act_.Identity, z_, m8_ if lo else m_)
        act(A("cf", c + 16, c + 22), A("cf", c, c + 6), act_.Identity, 16.0, 15.0)
    cp(A("inv", 0, 22 * len(kinds)), A("cf", 0, 22 * len(kinds)))
    for o in [A("zf", 0, 272), A("zf", 272, 544), A("zt", 0, 128), A("bt1", 0, 64), A("bt2", 0, 64), A("nb")]:
        copy(o, A("zf", 544, 544 + o[2]))
    for o in [A("pr"), R("pin", 0), R("pin", 1), R("pin", 2), A("rw")]:
        copy(o, A("ones", 0, o[2]))
    fill(A("dif"), -16.0)
    act(A("dif", 15, 256, 16), A("ones", 0, 16), act_.Identity, 240.0, m_)
    a, b = sorted(min(out_keys(t, 0, 1)[1][0][1]) for t in (1, 2))
    fill(A("kk", a, b + 1, b - a), -3e29)

    cp(A("sin", 0, 512, 32), A("lw", 16, 32))
    ts(A("gt1", 0, 17), A("lw", 16, 33), 496, op_.bitwise_and)
    ts(A("r4", 0, 1), A("lw", 32, 33), 4.0, op_.mult)
    scan(A("sb"), A("p32"), A("sin", 0, 512))
    tt(A("gt2", 0, 17), A("gt1", 0, 17), A("lw", 16, 33), op_.add)
    ts(A("rof", 0, 8, 2), A("ci", 0, 4), A("r4", 0, 1), op_.add)
    turn(A("str", 0, 512), A("sb"))
    ts(A("goff", 0, 17), A("gt2", 0, 17), h_, op_.add, -15.0, op_.add)
    ts(sp(0, 19, 9), A("ones", 0, 3), A("r4", 0, 1), op_.mult, 0.25, op_.mult)
    for b in range(4):
        act(A("zf", 1056 + b, 1120, 4), ind(A("xi"), A("rof", 2 * b, 2 * b + 1)))
    quant(*qr(0), A("zf", 608, 1120))
    send_root(0)
    urgent(UP0)
    behind = [("q", nxt["send"])]

    def table(k, n=257):
        return A("tt", TB * k, TB * k + n)

    cp(A("riu"), A("lw", 16, 32))
    act(table(1, 256), ind(A("str"), A("goff", 0, 16)))
    act(table(2, 256), ind(table(1), A("riu")))
    act(table(3, 256), ind(table(2), A("riu")))
    cp(A("sin", 0, 512, 32), A("lw", 0, 16))
    scan(A("sbl"), A("p32"), A("sin", 0, 512))
    turn(A("stl"), A("sbl"))
    act(table(4, 256), ind(A("stl"), A("gl")))
    act(table(0, 256), ind(A("str"), A("gl")))
    for b in range(4):
        act(plane(b, 0, 256), A("xi", b, 1024, 4), scale=0.5)
    quant(A("qu"), A("su"), A("ut"))
    words = ind(A("qu"), A("upl"), True)
    run("V", lambda: g.vector.tensor_copy(T.qu2[:].bitcast(dt.uint32), words[0]), [A("qu2")], [words], span(words, 1))
    act(A("su2"), ind(A("su"), A("upl")))
    const(R("xp", (0, 4), 256, 272), 0)
    keep(A("pp"), [[0, 16], [1, 16]], op_.is_ge, -2, after=behind)
    iota(R("cpa", (0, 3)), [[0, 3], [1, 8]], -5, after=behind)
    iota(A("c3", 0, 3), [[TB, 3]])
    const(A("pr", 15, 241, 15), -1, behind)
    const(A("pr", 0, 256, 16), 0, behind)
    const(R("gs", (0, 3), 256, 272), 1, behind)
    const(R("sc", 4, 95, 96), 256)
    const(A("hr", 64, 68), 0, behind)
    for t in range(3):
        const(A("cap", 16 * t, 16 * t + 16), 10 if low[t] else 2, behind)
        if low[t]:
            const(R("pin", t, 8, 256, 16), -15, behind)
            if t and PATCH:
                const(K(t, 0, 1), 0, behind)

    def look(row, j, win, off):
        lo, hi = 16 * j, 16 * (j + off[2])
        tt(R("mk", row, lo, hi), ind(win, off), A("mask", 0, hi - lo), op_.mult)
        scan(R("sc", row, lo, hi), A("p16", 0, hi - lo), R("mk", row, lo, hi))

    def end(row, j0, j1):
        return R("sc", row, 16 * j0 + 15, 16 * j1, 16)

    look(0, 0, A("str"), A("goff", 16, 17))
    ts(sp(1, 20, 18), A("ones", 0, 2), end(0, 0, 1), op_.mult)
    look(0, 1, table(1), sp(0, 2))
    cp(sp(2, 4), end(0, 1, 3))
    look(1, 0, table(3), sp(0, 4))
    cp(sp(4, 8), end(1, 0, 4))
    look(2, 0, table(4), sp(0, 2))
    for j in range(2):
        ts(A("wl", 3 * j, 3 * j + 3), A("c3", 0, 3), end(2, j, j + 1), op_.add)
    cp(sp(10, 21, 10), end(2, 0, 2))
    look(3, 0, table(0, 2 * TB + 257), A("wl", 0, 6))
    cp(A("wl", 6, 11), end(3, 0, 5))
    look(4, 0, table(2), A("wl", 6, 11))
    cp(sp(11, 17), end((3, 5), 0, 3))
    cp(sp(21, 27), end((3, 5), 3, 6))

    def spine_tile(t, off, i0, engines):
        for b in range(4):
            mul(engines[b], A("bt%d" % t, 64 * i0 + b, 64 * (i0 + off[2]), 4), ind(plane(b, 0, 272), off), 2.0)

    def keys(t, pen):
        i0, c = int(t > 0), 128 * t
        quant(*qb(t), A("bt%d" % t))
        mm(6, (A("qu2"), A("su2"), *qb(t)))
        km, ks = A("km", c + 16 * i0, c + 128), A("ks", c + 16 * i0, c + 128)
        tt(km, bank(6, 16 * i0, 128), A("mask", 16 * i0, 128), op_.mult)
        scan(ks, A("p16", 16 * i0, 128), km)
        s = A("ks", c + 16 * i0 + 15, c + 128, 16)
        tt(out_keys(t, i0, 8), s, pen, op_.add if low[t] else op_.subtract)
        send(t, "k", [(K(t, own[t], own[t] + 8), out_keys(t, 0, 8))], 0.0)
        if low[t]:
            tt(K(t, i0, 8), s, pen, op_.subtract)
        send_bulk(t)

    def unpack(t, q, s, to):
        for b in range(4):
            mm(b, (*qe(b), q, s))
        for b in range(4):
            act(A("dh%d" % t, 256 * b + to, 256 * b + to + 128), bank(b), scale=0.5)

    def pairs(t):
        for j in range(2):
            act(A("kx", 128 * j, 128 * j + 128), ind(K(t, 0, 16), A("maxl", 8 * j, 8 * j + 8)))
        for j in range(2):
            tt(A("gm", 128 * j, 128 * j + 128), ind(K(t, 0, 16), A("minl", 8 * j, 8 * j + 8)), A("kx", 128 * j, 128 * j + 128), op_.is_ge)

    def order(t):
        s = K(t, own[t], own[t] + 1)
        if not PATCH or not t:
            pairs(t)
        elif low[t]:
            ts(A("gm", 15, 256, 16), K(t, 0, 16), s, op_.is_le)
            ts(A("gm", 0, 15), K(t, 1, 16), s, op_.is_le)
        else:
            ts(A("gm", 7, 128, 16), K(t, 0, 8), s, op_.is_ge)
            ts(A("gm", 135, 256, 16), K(t, 8, 16), s, op_.is_le)
            ts(A("gm", 128, 135), K(t, 9, 16), s, op_.is_le)
            ts(A("gm", 136, 144), K(t, 0, 8), s, op_.is_ge)
        scan(R("gs", t, 0, 256), A("pr"), A("gm"))

    def insert(t):
        s, c = A("kr", 4 * t, 4 * t + 1), 32 * t - 32
        if low[t]:
            ts(A("nb", c, c + 8), K(t, 0, 8), s, op_.is_lt, -1.0, op_.mult)
            ts(A("nb", c + 8, c + 16), K(t, 8, 16), s, op_.is_le, -1.0, op_.mult)
        else:
            ts(A("nb", c, c + 16), K(t, 0, 16), s, op_.is_le, -1.0, op_.mult)

    def ranks(t):
        c = 32 * t - 32
        tt(A("rw", c, c + 16), R("gs", t, 15, 256, 16), A("nb", c, c + 16), op_.subtract)
        return A("rw", c, c + 32)

    at = [0]

    def invert(have, wants, out):
        lo = at[0]
        for want in wants:
            tt(A("nm", at[0], at[0] + want[2]), have, want, op_.not_equal)
            at[0] += want[2]
        scan(A("iv", lo, at[0]), A("nm", lo, at[0]), A("dif", 0, at[0] - lo))
        cp(out, A("iv", lo + 15, at[0], 16))

    def wanted(t, i0, i1):
        return [A("pe", 256 * t + c + 16 * i0, 256 * t + c + 16 * i1) for c in (0, 128)]

    def window(t, b):
        return A("dh%d" % t, 256 * b, 256 * b + 256)

    def layer(t, i0, la, ln, buf, c, tile, j, k0):
        n = 16 * la[2]
        q, s = A("qz", 128 * j, 128 * j + 128), A("sz", 128 * j, 128 * j + 128)
        for b in range(4):
            act(A(buf, c + n * b, c + n * b + n), ind(window(t, b), la))
        for b in range(4):
            tt(A(tile, 64 * i0 + b, 64 * i0 + 4 * n, 4), ind(window(t, b), ln), A(buf, c + n * b, c + n * b + n), op_.add)
        quant(q, s, A(tile, 0, 512))
        for b in range(4):
            mm(k0 + b, (*qw(b), q, s))

    def relu(eng, o, i, c):
        if eng == "S":
            act(o, i, act_.Relu, scale=c)
        else:
            ts(o, i, 0.0, op_.max, c, op_.mult)

    def short_road(t, la, ln):
        n = 16 * la[2]
        w = 8 * n + 8
        for b in range(4):
            act(A("ef", b, 4 * n, 4), ind(window(t, b), la))
        for b in range(4):
            tt(A("zf", 24 + b, 32 * n, 32), ind(window(t, b), ln), A("ef", b, 4 * n, 4), op_.add)
        act(A("ei"), A("ef", 0, 64), scale=2.0)
        quant(A("qf", 0, w), A("sf", 0, w), A("zf", 0, 4 * w))
        for i in range(la[2]):
            c = [128 * i + 6 - 2 * b for b in range(4)]
            mm(4 + i, *[(*qw(b), A("qf", c[b], c[b] + 128), A("sf", c[b], c[b] + 128)) for b in range(4)])
        relu(RELU, A("rf", 0, 64), bank(4, 0, 128, 2), 0.03125)
        tt(A("bt%d" % (t + 1), 0, 64), A("rf", 0, 64), A("ei"), op_.add)
        quant(*qr(t + 1), A("bt%d" % (t + 1)))
        send_root(t + 1)
        mm(7, (A("qu2"), A("su2"), *qr(t + 1)))
        tt(A("kq"), bank(7, 0, 16), A("mask", 0, 16), op_.mult)
        mine = K(t + 1, own[t + 1], own[t + 1] + 1)
        red(mine, A("kq"))
        send(t + 1, "s", [(A("kr", 4 * t + 4, 4 * t + 5), mine)], 0.0)

    def long_road(t, la, ln, k0, after):
        i0, hi = FAST[t], [368, 480][t]
        n = 16 * (8 - i0)
        layer(t, i0, la, ln, "eh%d" % t, 0, "zt", 1, k0)
        o = R("xp", (0, 4), hi - n, hi)
        for b in range(4):
            relu("S", plane(b, hi - n, hi), bank(k0 + b, 128 - n, 128), 0.015625)
            if ADD[t] == "V":
                tt(plane(b, hi - n, hi), plane(b, hi - n, hi), A("eh%d" % t, n * b, n * b + n), op_.add)
        if ADD[t] == "G":
            dma("G", o[0], T["eh%d" % t][:], o[1], A("eh%d" % t)[1], 1.5, after=after, accum_op=op_.add)

    def scatter(lo, hi, v0):
        o = ind(A("iw"), A("so", lo, hi))
        i = A("val", v0, v0 + 16 * (hi - lo))
        run("V", lambda: g.vector.tensor_copy(o[0], i[0]), [A("iw")], [i, A("so", lo, hi)], (0.06, "s", i[2]))

    def off(lo, hi, st=1):
        return A("off", lo, hi, st)

    spine_tile(0, sp(0, 8), 0, B0)
    ts(A("pen0"), sp(0, 8), 256.0, op_.is_equal, BIG, op_.mult)
    keys(0, A("pen0"))
    behind = [("q", nxt["send"])]
    iota(A("val", 0, 16), [[1, 16]], 480, after=behind)
    iota(A("val", 16, 32), [[-1, 16]], -496, after=behind)
    iota(A("val", 32, 240), [[1, 208]], 272, after=behind)
    iota(A("val", 240, 336), [[1, 96]], 512, after=behind)
    iota(A("iw", 0, 256), [[1, 256]], after=behind)
    copy(A("iw", 256, 512), A("iw", 0, 256))
    iota(A("s3"), [[0, 3], [16, 9]], 256, after=behind)
    act(A("dum"), A("s3"), act_.Identity, 1.0, m_)
    unpack(0, *qb(0), 128)
    cp(A("s1"), sp(0, 28))
    act(R("pen", (0, 3)), A("s1", 0, 27), act_.Relu, BIG, -255.0 * BIG)
    act(R("fn", (0, 3)), A("s1", 1, 28), act_.Sign, -1.0, 256.0)
    tt(R("pq", (0, 3), 0, 8), R("pen", (0, 3), 0, 8), R("cpa", (0, 3)), op_.add)
    tt(R("pq", (0, 3), 8, 16), R("pq", (0, 3), 0, 8), R("fn", (0, 3), 0, 8), op_.add)
    tt(R("pin", (0, 3), 1, 256, 16), R("pq", (0, 3)), A("cap"), op_.min)
    for t in range(3):
        scan(A("pe", 256 * t, 256 * t + 256), A("pp"), R("pin", t))
    spine_tile(1, sp(10, 17), 1, "SSSS")
    keys(1, R("pen", 1, 1, 8))
    ts(A("r4", 1, 2), sp(1, 2), 256.0, op_.not_equal, bm_, op_.mult)
    ts(A("ob", 0, 8, 2), A("ci", 0, 4), A("r4", 1, 2), op_.add, 64.0, op_.add)
    spine_tile(2, sp(20, 26), 2, "SSSS")
    order(0)
    if PATCH:
        pairs(1)
    unpack(0, *far(0), 0)
    invert(ind(R("gs", 0), ends(0, 2)), wanted(0, 0, 2), off(0, 4))
    short_road(0, off(0, 2), off(2, 4))

    load("Y", A("vt"), T.v[:], 0.7, A("kq")[1])
    order(1)
    unpack(1, *qr(1), 128)
    relu("S", A("rf", 64, 128), bank(5, 0, 128, 2), 0.015625)
    tt(A("hr", 0, 64), A("rf", 64, 128), A("ef", 64, 128), op_.add)
    for b in range(4):
        act(A("bt2", 64 + b, 128, 4), ind(A("hr"), A("ob", 2 * b, 2 * b + 1)), scale=2.0)
    keys(2, R("pen", 2, 1, 8))
    behind = [("q", nxt["send"])]
    for j, want in enumerate(wanted(1, 0, 1)):
        tt(A("pk", 16 * j, 16 * j + 16), ind(R("gs", 1), ends(1, 1)), want, op_.subtract)
    if PATCH:
        pairs(2)
    unpack(1, *far(1), 0)
    insert(1)
    invert(ind(A("nb", 0, 32), inv(1, 2)), [A("pk")], off(4, 8, 2))
    short_road(1, off(4, 5), off(6, 7))

    f1, f3, f4, f5 = [A("ff", 16 * j, 16 * j + 16) for j in range(4)]
    tt(A("s2"), A("s1", 0, 27), R("pen", (0, 3)), op_.add)
    tt(A("s3"), A("s2"), A("dum"), op_.min)
    cp(A("so", 0, 27), A("s3"))
    scatter(0, 8, 0)
    scatter(10, 17, 128)
    scatter(20, 26, 240)
    for h in range(2):
        dma("Y", T.tw[:, 16 * h:16 * h + 16], T.iw[16 * h::32, :], A("tw", 16 * h, 16 * h + 16)[1], A("iw")[1], 0.5)
    turn(A("wr"), A("tw"))
    urgent(6.0)
    act(f1, A("wr", 0, 16), act_.Abs)
    cp(A("fo"), f1)
    ts(f3, A("wr", 0, 16), 272.0, op_.is_ge)
    tt(f4, A("lw", 16, 32), A("lw", 0, 16), op_.subtract)
    tt(f5, f3, f4, op_.mult)
    tt(A("ow", 0, 16), A("lw", 0, 16), f5, op_.add)
    tt(A("ow", 16, 32), A("lw", 16, 32), f5, op_.subtract)
    turn(A("olt"), A("ow"))
    for h in range(2):
        dma("Y", T.ol[h::2, :], T.olt[:, 16 * h:16 * h + 16], ins=A("olt")[1], more=1.0)

    order(2)
    invert(ind(R("gs", 0), ends(0, 6)), wanted(0, 2, 8), off(8, 20))
    long_road(0, off(8, 14), off(14, 20), 0, behind)
    unpack(2, *qr(2), 128)
    invert(ind(ranks(1), inv(1, 16)), [A("pe", 256, 512)], off(21, 37))
    long_road(1, off(22, 29), off(30, 37), 4, [("q", nxt["send"])])
    quant(A("qv"), A("sv"), A("vt"))
    unpack(2, *far(2), 0)
    insert(2)
    rw = ranks(2)
    for h in range(2):
        k0, c = 4 - 4 * h, 40 + 8 * h
        invert(ind(rw, inv(2, 4)), wanted(2, 4 * h, 4 * h + 4), off(c, c + 8))
        layer(2, 4 * h, off(c, c + 4), off(c + 4, c + 8), "eh2", 256 * h, ["zf", "zt"][h], h, k0)
        for b in range(4):
            c = 256 * h + 64 * b
            relu("S", A("rb", c, c + 64), bank(k0 + b, 64 * h, 64 * h + 64), 0.015625)
            tt(plane(b, 480 + 64 * h, 544 + 64 * h), A("rb", c, c + 64), A("eh2", c, c + 64), op_.add)
    for h in range(2):
        c = 128 * h
        for b in range(4):
            mul(LAST[h][b], A("xt", 4 * c + b, 4 * c + 512, 4), ind(plane(b, 0, PL), A("fo", 8 * h, 8 * h + 8)), 2.0)
        q, s = A("qx", c, c + 128), A("sx", c, c + 128)
        quant(q, s, A("xt", 4 * c, 4 * c + 512))
        mm(4 + h, (A("qv"), A("sv"), q, s))
        dma("Y", T.oc[:, 4 * c:4 * c + 512], raw(q)[0], ins=q[1], more=0.5)
        act(A("ys", c, c + 128), bank(4 + h))
        dma("S", T.y[:, c:c + 128], T.ys[:, c:c + 128], ins=A("ys", c, c + 128)[1], more=0.5)
    for k in range(4):
        dma("Y", T.osc[4 * k:4 * k + 4, :], T.sx[32 * k:32 * k + 4, :], ins=A("sx")[1])

    total, direct, token, known, last = dict(arrive), {}, {}, {q: {} for q in queue}, {}
    for pos, k in enumerate(polish(ops, sent, arrange(ops, sent))):
        o = ops[k]
        mine = known[o["eng"]]
        need = [(d[1], arrive[d[1]], {}, j) if isinstance(d, tuple) else token[d] for j, d in enumerate(sorted(o["deps"], key=str))
                if not (isinstance(d, tuple) and d[0] == "q")]
        for s, v, earlier, _ in sorted(need, key=lambda x: -x[3]):
            if mine.get(s, 0) < v:
                queue[o["eng"]].wait_ge(T.sem[s], v)
                direct[s] = max(direct.get(s, 0), v)
                mine[s] = v
                for s2, v2 in earlier.items():
                    mine[s2] = max(mine.get(s2, 0), v2)
        s = o["sem"] or "c" + o["eng"]
        total[s] = total.get(s, 0) + o["n"]
        token[k] = (s, total[s], dict(mine), 1000 + pos)
        last[s] = pos + (50 if o["lag"] else 0)
        o["call"](s)
    for s in sorted(total, key=lambda s: (last.get(s, 0), s)):
        if direct.get(s, 0) < total[s]:
            g.wait_ge(T.sem[s], total[s])
